import numpy as np
import ml_dtypes


def mxq(x, axis, fmt="e4m3"):
    dtype, down = {"e4m3": (ml_dtypes.float8_e4m3fn, 7), "e5m2": (ml_dtypes.float8_e5m2, 14)}[fmt]
    v = np.moveaxis(np.asarray(x, np.float32).astype(ml_dtypes.bfloat16).astype(np.float64), axis, -1)
    blocks = v.reshape(v.shape[:-1] + (-1, 32))
    amax = np.abs(blocks).max(-1, keepdims=True)
    byte = np.maximum(np.where(amax > 0, np.frexp(amax)[1] - 1 + 127, 0) - down, 1)
    scale = np.exp2(byte - 127.0)
    codes = (blocks / scale).astype(np.float32).astype(dtype).astype(np.float64)
    return np.moveaxis((codes * scale).reshape(v.shape), -1, axis)


WIDE = False


def mx_kscale(k):
    if not WIDE:
        return np.ones(k)
    levels = np.array([10, -10, 5, -5, 0])
    if k % 512:
        return np.exp2(np.random.permutation(np.resize(levels, k // 32))).repeat(32)
    a = np.empty((k // 512, 16))
    for p in range(k // 512):
        a[p, :8] = np.random.permutation(np.resize(levels, 8))
        for g in range(8):
            far = levels[np.abs(levels - a[p, g]) >= 10]
            a[p, g + 8] = far[np.random.randint(len(far))]
    return np.exp2(a.ravel()).repeat(32)


BF16 = ml_dtypes.bfloat16


def bf(x):
    return np.asarray(x, np.float32).astype(BF16)


def f64(x):
    return np.asarray(x).astype(np.float64)


E2M1 = np.array([0.0, 0.5, 1.0, 1.5, 2.0, 3.0, 4.0, 6.0, -0.0, -0.5, -1.0, -1.5, -2.0, -3.0, -4.0, -6.0])


def pack_weight(w, fmt):
    k, n = w.shape
    w = f64(bf(w)).reshape(k // 32, 32, n)
    amax = np.abs(w).max(1)
    if fmt == "e4m3":
        byte = np.frexp(amax)[1] - 1 + 127 - 7
    else:
        mant, ex = np.frexp(amax / 6.0)
        byte = np.where(mant > 0.5, ex, ex - 1) + 127
    byte = np.clip(np.where(amax > 0, byte, 1), 1, 254)
    scaled = (w * np.exp2(127.0 - byte)[:, None, :]).reshape(k, n).astype(np.float32)
    by_word = np.ascontiguousarray(scaled.reshape(k // 512, 128, 4, n).transpose(0, 1, 3, 2))
    if fmt == "e4m3":
        words = by_word.astype(ml_dtypes.float8_e4m3fn).view(np.uint8)
    else:
        c = by_word.astype(ml_dtypes.float4_e2m1fn).view(np.uint8) & 0xF
        words = c[..., 0::2] | (c[..., 1::2] << 4)
    return np.ascontiguousarray(words), np.ascontiguousarray(byte.astype(np.uint8).reshape(k // 512, 16, n))


def unpack_weight(words, scales, fmt):
    g, p, n, _ = words.shape
    if fmt == "e4m3":
        vals = np.ascontiguousarray(words).view(ml_dtypes.float8_e4m3fn).astype(np.float64)
    else:
        nib = np.empty((g, p, n, 4), np.uint8)
        nib[..., 0::2] = words & 0xF
        nib[..., 1::2] = words >> 4
        vals = E2M1[nib]
    vals = vals * np.repeat(np.exp2(scales.astype(np.float64) - 127.0), 8, axis=1)[..., None]
    return vals.transpose(0, 1, 3, 2).reshape(g * 512, n)
def pack4(w):
    words, scales = pack_weight(w, "e2m1")
    return words.reshape(words.shape[0], 128, -1), scales


def unpack4(words, scales):
    return unpack_weight(words.reshape(words.shape[0], 128, -1, 2), scales, "e2m1")


def planes(Y):
    n, m = Y.shape
    b = f64(bf(Y)).reshape(n // 32, 32, m)
    amax = np.abs(b).max(1)
    byte = np.clip(np.where(amax > 0, np.frexp(amax)[1] - 1 + 127 - 7, 1), 1, 254)
    codes = (b * np.exp2(127.0 - byte)[:, None, :]).reshape(n, m).astype(np.float32).astype(ml_dtypes.float8_e4m3fn).view(np.uint8)
    words = codes.reshape(n // 512, 128, 4, m).transpose(0, 1, 3, 2)
    return np.ascontiguousarray(words), np.ascontiguousarray(byte.astype(np.uint8).reshape(n // 512, 16, m))


M, K, N = 768, 1024, 1536


def setup_inputs():
    s = mx_kscale(K)[:, None]
    col = np.exp(0.8 * np.random.randn(N))
    size = 0.5 * col / np.sqrt(K)
    d = bf(np.exp(0.3 * np.random.randn(K)))
    dk = f64(d)[:, None]
    ea_words, ea_scales = pack_weight(np.random.randn(K, M) / s, "e4m3")
    old_words, old_scales = pack4(np.random.randn(K, N) * size / dk * s)
    mid_words, mid_scales = pack_weight(np.random.randn(K, N) * size / dk * s, "e4m3")
    e_new = bf(np.random.randn(K, N) * size * s)
    f = bf(np.random.uniform(0.4, 0.9, N))
    b = bf(0.5 * col * np.random.randn(M, N))
    return {"ea_words": ea_words, "ea_scales": ea_scales, "old_words": old_words, "old_scales": old_scales,
            "mid_words": mid_words, "mid_scales": mid_scales, "e_new": e_new, "d": d, "f": f, "b": b}

def reference(ea_words, ea_scales, old_words, old_scales, mid_words, mid_scales, e_new, d, f, b):
    ea = unpack_weight(ea_words, ea_scales, "e4m3")
    wo = unpack4(old_words, old_scales)
    wm = unpack_weight(mid_words, mid_scales, "e4m3")
    wn = mxq(f64(e_new) / f64(d)[:, None], 0, "e4m3")
    p_new = ea.T @ wn
    p_mid = ea.T @ wm
    p_old = ea.T @ wo
    y = f64(b) - (p_new + p_mid + f64(f) * p_old)
    Y = y.T
    words, scales = planes(Y)
    return y, words, scales

@@ -1,0 +1,375 @@
+from contextlib import ExitStack
+
+import concourse.mybir as mybir
+from concourse.masks import make_identity
+
+M, K, N = 768, 1024, 1536
+FLOPS = 3 * 2 * M * K * N
+
+F32 = mybir.dt.float32
+BF16 = mybir.dt.bfloat16
+I32 = mybir.dt.int32
+U32 = mybir.dt.uint32
+U8 = mybir.dt.uint8
+FP8X4 = mybir.dt.float8_e4m3fn_x4
+FP4X4 = mybir.dt.float4_e2m1fn_x4
+ALU = mybir.AluOpType
+
+P = 128
+PACK = 4
+W = 512
+PASSES = K // (P * PACK)
+GROUPS = N // W
+ROWS = M // P
+TILES = GROUPS * ROWS
+BANKS = 8
+LEAD = 3
+T_BUFS = 6
+YB_BUFS = 10
+EA_FIRST = 3
+MID_ROW = 4
+NEW_FIRST = 3
+ON_G = lambda n: n % 2 == 0 and n > 0
+
+
+def tile_schur_window_block_k3_kernel(
+    tc, ea_words, ea_scales, old_words, old_scales, mid_words, mid_scales, e_new, d, f, b, out_0, out_1, out_2
+):
+    nc = tc.nc
+    with ExitStack() as ctx:
+        sb = ctx.enter_context(tc.tile_pool(name="sb", bufs=1))
+        ps = ctx.enter_context(tc.psum_pool(name="ps", bufs=1))
+        ctx.enter_context(tc.manual_schedule())
+
+        def tiles(name, count, shape, dtype):
+            return [sb.tile(shape, dtype, name="%s%d" % (name, i), align_bytes=64) for i in range(count)]
+
+        banks = [ps.tile([P, W], F32, name="bank%d" % i) for i in range(BANKS)]
+        ident = sb.tile([P, P], F32, name="ident", align_bytes=64)
+        d_sb = sb.tile([P, PASSES, PACK], BF16, name="d_sb", align_bytes=64)
+        d_inv = sb.tile([P, PASSES * PACK], F32, name="d_inv", align_bytes=64)
+        f_sb = sb.tile([P, GROUPS, PACK], BF16, name="f_sb", align_bytes=64)
+        f_all = sb.tile([P, N], BF16, name="f_all", align_bytes=64)
+        in_planes_ea = sb.tile([P, PASSES, M], U8, name="in_planes_ea", align_bytes=64)
+        in_planes_w = sb.tile([P, PASSES, N], U8, name="in_planes_w", align_bytes=64)
+        in_planes_mid = sb.tile([P, PASSES, N], U8, name="in_planes_mid", align_bytes=64)
+        rest = sb.tile([P, W], F32, name="rest", align_bytes=64)
+        ea = sb.tile([P, PASSES, M], U32, name="ea", align_bytes=64)
+        old = tiles("old", GROUPS, [P, PASSES, 2 * W], U8)
+        mid = tiles("mid", GROUPS, [P, PASSES, W], U32)
+        raw = tiles("raw", GROUPS * PASSES, [P, PACK, W], BF16)
+        scaled = tiles("scaled", 2, [P, PACK, W], BF16)
+        woven = tiles("woven", 2, [P, W, PACK], BF16)
+        new = tiles("new", GROUPS * PASSES, [P, W], U32)
+        new_plane = tiles("new_plane", GROUPS * PASSES, [P, W], U8)
+        b_sb = tiles("b_sb", GROUPS, [P, ROWS, W], BF16)
+        part = tiles("part", T_BUFS, [P, W], F32)
+        y = tiles("y", TILES, [P, W], F32)
+        y_bf = tiles("y_bf", YB_BUFS, [P, W], BF16)
+        y_t = tiles("y_t", 4, [P, 2 * P, PACK], BF16)
+        out_words = tiles("out_words", GROUPS, [P, M], U32)
+        out_plane = tiles("out_plane", GROUPS, [P, M], U8)
+
+        taken = []
+        bank_of = {}
+
+        def take_bank(key):
+            bank_of[key] = banks[len(taken) % BANKS]
+            taken.append(key)
+            return bank_of[key]
+
+        def cols(g):
+            return slice(g * W, (g + 1) * W)
+
+        ea_src = ea_words.rearrange("c p m t -> p c (m t)").bitcast(I32)
+        old_src = old_words.rearrange("c p x -> p c x").bitcast(I32)
+        mid_src = mid_words.rearrange("c p n t -> p c (n t)").bitcast(I32)
+        e_src = e_new.rearrange("(c p t) n -> c p t n", p=P, t=PACK)
+        b_src = b.rearrange("(a p) n -> p a n", p=P)
+
+        def load_ea(a0, a1, queue=nc.sync):
+            queue.dma_start(out=ea[:, :, a0 * P : a1 * P].bitcast(I32), in_=ea_src[:, :, a0 * P : a1 * P])
+
+        def load_old(g, queue=nc.sync):
+            queue.dma_start(out=old[g][:].bitcast(I32), in_=old_src[:, :, g * W // 2 : (g + 1) * W // 2])
+
+        def load_mid(g):
+            nc.sync.dma_start(out=mid[g][:].bitcast(I32), in_=mid_src[:, :, cols(g)])
+
+        def load_e(g, c, queue=nc.sync):
+            queue.dma_start(out=raw[g * PASSES + c][:], in_=e_src[c][:, :, cols(g)])
+
+        def load_b(g, a0, a1):
+            nc.sync.dma_start(out=b_sb[g][:, a0:a1, :], in_=b_src[:, a0:a1, cols(g)])
+
+        def load_plane(queue, plane, row0, scales, q0, q1, x0, x1):
+            src = scales.rearrange("c q n -> q c n").bitcast(I32)
+            for quad in range(q0, q1):
+                row = 32 * quad + row0
+                queue.dma_start(
+                    out=plane[row : row + 4, :, x0:x1].bitcast(I32), in_=src[4 * quad : 4 * quad + 4, :, x0 // 4 : x1 // 4]
+                )
+
+        def scale_rows(g, c):
+            s = g * PASSES + c
+            for t in range(PACK):
+                k = c * PACK + t
+                nc.vector.tensor_scalar(
+                    out=scaled[s % 2][:, t, :], in0=raw[s][:, t, :], scalar1=d_inv[:, k : k + 1], scalar2=None, op0=ALU.mult
+                )
+
+        def weave(g, c, half, engine):
+            s = g * PASSES + c
+            h = slice(half * W // 2, (half + 1) * W // 2)
+            dst = woven[s % 2][:, h, :].rearrange("p (c i) t -> p c t i", i=4)
+            src = scaled[s % 2][:, :, h].rearrange("p t (c i) -> p c t i", i=4)
+            if engine == "scalar":
+                nc.scalar.copy(out=dst, in_=src)
+            else:
+                nc.vector.tensor_copy(out=dst, in_=src)
+
+        def quantize_new(g, c):
+            s = g * PASSES + c
+            nc.vector.quantize_mx(
+                out=new[s][:].bitcast(FP8X4), scales=new_plane[s][:], in_=woven[s % 2][:].rearrange("p w t -> p (w t)")
+            )
+
+        def mx(key, n, c, rhs, rhs_scale, start, stop):
+            a = n % ROWS
+            nc.tensor.matmul_mx(
+                out=bank_of[key][:],
+                lhsT=ea[:, c, a * P : (a + 1) * P].bitcast(FP8X4),
+                lhsT_scale=in_planes_ea[:, c, a * P : (a + 1) * P],
+                rhs=rhs,
+                rhs_scale=rhs_scale,
+                start=start,
+                stop=stop,
+            )
+
+        def mm_old(n):
+            g = n // ROWS
+            take_bank(("old", n))
+            for c in range(PASSES):
+                mx(("old", n), n, c, old[g][:, c, :].bitcast(FP4X4), in_planes_w[:, c, cols(g)], c == 0, c == PASSES - 1)
+
+        def mm_mid(n):
+            g = n // ROWS
+            if n >= NEW_FIRST:
+                take_bank(("sum", n))
+            for c in range(PASSES):
+                mx(("sum", n), n, c, mid[g][:, c, :].bitcast(FP8X4), in_planes_mid[MID_ROW:, c, cols(g)], c == 0 and n >= NEW_FIRST, False)
+
+        def mm_new(n, c):
+            s = n // ROWS * PASSES + c
+            opens = c == 0 and n < NEW_FIRST
+            if opens:
+                take_bank(("sum", n))
+            mx(("sum", n), n, c, new[s][:].bitcast(FP8X4), new_plane[s][:], opens, c == PASSES - 1)
+
+        def weigh_old(n):
+            nc.vector.tensor_tensor(
+                out=part[n % T_BUFS][:], in0=bank_of[("old", n)][:], in1=f_all[:, cols(n // ROWS)], op=ALU.mult
+            )
+
+        def remainder(n):
+            return rest if ON_G(n) else part[n % T_BUFS]
+
+        def from_b(n):
+            eng = nc.gpsimd if ON_G(n) else nc.vector
+            eng.tensor_tensor(
+                out=remainder(n)[:], in0=b_sb[n // ROWS][:, n % ROWS, :], in1=part[n % T_BUFS][:], op=ALU.subtract
+            )
+
+        def finish(n):
+            nc.vector.tensor_tensor(out=y[n][:], in0=remainder(n)[:], in1=bank_of[("sum", n)][:], op=ALU.subtract)
+
+        def round_y(n):
+            nc.scalar.copy(
+                out=y_bf[n % YB_BUFS][:].rearrange("p (u j e) -> p u j e", u=2, e=2),
+                in_=y[n][:].rearrange("p (j u e) -> p u j e", u=2, e=2),
+            )
+
+        def turn(n0, count):
+            bank = take_bank(("turn", n0))
+            for h in range(count):
+                words = y_bf[(n0 + h) % YB_BUFS][:].bitcast(F32)
+                for u in range(2):
+                    o = (count * u + h) * P
+                    nc.tensor.transpose(bank[:, o : o + P], words[:, u * P : (u + 1) * P], ident[:])
+
+        def copy_turned(n0, count):
+            nc.scalar.copy(
+                out=y_t[(n0 + 1) // 2 % 4][:, : count * P, :].rearrange("p m t -> p (m t)").bitcast(F32).rearrange("p (m u) -> p m u", u=2),
+                in_=bank_of[("turn", n0)][:, : 2 * count * P].rearrange("p (u m) -> p m u", u=2),
+            )
+
+        def quantize_y(n0, count):
+            g, m0 = n0 // ROWS, n0 % ROWS * P
+            nc.vector.quantize_mx(
+                out=out_words[g][:, m0 : m0 + count * P].bitcast(FP8X4),
+                scales=out_plane[g][:, m0 : m0 + count * P],
+                in_=y_t[(n0 + 1) // 2 % 4][:, : count * P, :].rearrange("p m t -> p (m t)"),
+            )
+
+        def round_last(n):
+            nc.vector.tensor_tensor(
+                out=y_bf[n % YB_BUFS][:].rearrange("p (u j e) -> p u j e", u=2, e=2),
+                in0=remainder(n)[:].rearrange("p (j u e) -> p u j e", u=2, e=2),
+                in1=bank_of[("sum", n)][:].rearrange("p (j u e) -> p u j e", u=2, e=2),
+                op=ALU.subtract,
+            )
+
+        def store_y(n):
+            a = n % ROWS
+            nc.sync.dma_start(out=out_0[a * P : (a + 1) * P, cols(n // ROWS)], in_=y[n][:])
+
+        def store_words(g, m0, m1):
+            dst = out_1[g].rearrange("p m t -> p (m t)").bitcast(I32)
+            nc.sync.dma_start(out=dst[:, m0:m1], in_=out_words[g][:, m0:m1].bitcast(I32))
+
+        def store_plane(g, queues):
+            for quad in range(4):
+                queues[quad].dma_start(
+                    out=out_2[g][4 * quad : 4 * quad + 4, :].bitcast(I32),
+                    in_=out_plane[g][32 * quad : 32 * quad + 4, :].bitcast(I32),
+                )
+
+
+        nc.vector.memset(in_planes_ea[:].rearrange("p c m -> p (c m)").bitcast(I32), 0)
+        nc.vector.memset(in_planes_w[:].rearrange("p c n -> p (c n)").bitcast(I32), 0)
+        make_identity(nc, ident[:])
+        nc.sync.dma_start(out=d_sb[:], in_=d.rearrange("(c p t) -> p c t", p=P, t=PACK))
+        nc.sync.dma_start(out=f_sb[:], in_=f.rearrange("(g p t) -> p g t", p=P, t=PACK))
+        nc.vector.memset(in_planes_mid[:].rearrange("p c n -> p (c n)").bitcast(I32), 0)
+        load_e(0, 0)
+        load_plane(nc.sync, in_planes_ea, 0, ea_scales, 0, 4, 0, M)
+        load_ea(0, EA_FIRST)
+        load_old(0)
+        load_plane(nc.sync, in_planes_w, 0, old_scales, 0, 4, 0, W)
+        load_e(0, 1)
+        load_mid(0)
+        load_plane(nc.sync, in_planes_mid, MID_ROW, mid_scales, 0, 4, 0, N)
+        load_b(0, 0, 2)
+        load_ea(EA_FIRST, ROWS)
+        load_e(1, 0)
+        load_plane(nc.sync, in_planes_w, 0, old_scales, 0, 4, W, N)
+        load_b(0, 2, ROWS)
+        load_e(1, 1)
+        load_old(1)
+        load_mid(1)
+        load_b(1, 0, ROWS)
+        load_e(2, 0)
+        load_e(2, 1)
+        load_old(2)
+        load_mid(2)
+        load_b(2, 0, ROWS)
+
+        nc.vector.reciprocal(out=d_inv[:], in_=d_sb[:].rearrange("p c t -> p (c t)"))
+        f_words = f_sb[:].rearrange("p g t -> p (g t)").bitcast(F32)
+        f_banks = [take_bank(("f", 0)), take_bank(("f", 1))]
+        for w in range(2 * GROUPS):
+            o = w % 4 * P
+            nc.tensor.transpose(f_banks[w // 4][:, o : o + P], f_words[:, w : w + 1].to_broadcast([P, P]), ident[:])
+
+        def spread_f(g):
+            o = g % 2 * 2 * P
+            nc.scalar.copy(
+                out=f_all[:, cols(g)].bitcast(F32).rearrange("p (j u) -> p j u", u=2),
+                in_=f_banks[g // 2][:, o : o + 2 * P].rearrange("p (u j) -> p j u", u=2),
+            )
+
+        spread_f(0)
+        mm_old(0)
+        mm_old(1)
+        scale_rows(0, 0)
+        weave(0, 0, 0, "scalar")
+        weave(0, 0, 1, "vector")
+        spread_f(1)
+        spread_f(2)
+        quantize_new(0, 0)
+        for n in range(NEW_FIRST):
+            mm_new(n, 0)
+        mm_old(2)
+        scale_rows(0, 1)
+        weave(0, 1, 0, "scalar")
+        weigh_old(0)
+        weave(0, 1, 1, "vector")
+        for n in range(NEW_FIRST):
+            mm_mid(n)
+        weigh_old(1)
+        from_b(0)
+        quantize_new(0, 1)
+        weigh_old(2)
+        from_b(2)
+
+        TURN = {2: [0], 8: [2, 4, 6], 12: [8, 10], 14: [12]}
+        scale_rows(1, 0)
+        for a in range(0, TILES, 2):
+            g, k = a // ROWS + 1, a % ROWS // 2
+            prep = g < GROUPS
+            last = a == TILES - 2
+            due = TURN.get(a - 2, [])
+            for n in (a, a + 1):
+                if n >= NEW_FIRST:
+                    mm_mid(n)
+                    mm_new(n, 0)
+                if n == TILES - 1:
+                    turn(a - 2, 2)
+                mm_new(n, 1)
+                if n == a:
+                    for m in (a + 3, a + 4):
+                        if m < TILES:
+                            mm_old(m)
+            for q in TURN.get(a, []):
+                turn(q, 2)
+            if prep and k < PASSES:
+                weave(g, k, 0, "scalar")
+            for q in due:
+                copy_turned(q, 2)
+            finish(a)
+            if 0 < a < TILES - 2:
+                from_b(a + 2)
+            if not last:
+                from_b(a + 1)
+            else:
+                for q in due:
+                    quantize_y(q, 2)
+                copy_turned(a - 2, 2)
+            round_y(a)
+            if prep and k < PASSES:
+                weave(g, k, 1, "scalar")
+            for m in (a + 3, a + 4):
+                if m < TILES:
+                    weigh_old(m)
+            if last:
+                round_last(a + 1)
+            finish(a + 1)
+            if not last:
+                round_y(a + 1)
+            if a == TILES - 4:
+                from_b(TILES - 1)
+            if prep and k == 0:
+                scale_rows(g, 1)
+            if g + 1 < GROUPS and k == 2:
+                scale_rows(g + 1, 0)
+            if not last:
+                for q in due:
+                    quantize_y(q, 2)
+            if prep and k < PASSES:
+                quantize_new(g, k)
+            store_y(a)
+            store_y(a + 1)
+            for q in due:
+                if q % ROWS == ROWS - 2:
+                    store_words(q // ROWS, 0, M)
+                    store_plane(q // ROWS, [nc.sync] * 4)
+        turn(16, 1)
+        turn(17, 1)
+        quantize_y(14, 2)
+        store_words(2, 0, 4 * P)
+        copy_turned(16, 1)
+        copy_turned(17, 1)
+        quantize_y(16, 1)
+        quantize_y(17, 1)
+        store_words(2, 4 * P, 6 * P)
+        store_plane(2, [nc.scalar, nc.sync, nc.scalar, nc.sync])

@@ -22,14 +22,11 @@ PASSES = K // (P * PACK)
 GROUPS = N // W
 ROWS = M // P
 TILES = GROUPS * ROWS
+PAIRS = TILES // 2
 BANKS = 8
-LEAD = 3
-T_BUFS = 6
-YB_BUFS = 10
-EA_FIRST = 3
+FIRST = 3
 MID_ROW = 4
-NEW_FIRST = 3
-ON_G = lambda n: n % 2 == 0 and n > 0
+POOL_COLS = 640
 
 
 def tile_schur_window_block_k3_kernel(
@@ -50,36 +47,41 @@ def tile_schur_window_block_k3_kernel(
         d_inv = sb.tile([P, PASSES * PACK], F32, name="d_inv", align_bytes=64)
         f_sb = sb.tile([P, GROUPS, PACK], BF16, name="f_sb", align_bytes=64)
         f_all = sb.tile([P, N], BF16, name="f_all", align_bytes=64)
-        in_planes_ea = sb.tile([P, PASSES, M], U8, name="in_planes_ea", align_bytes=64)
-        in_planes_w = sb.tile([P, PASSES, N], U8, name="in_planes_w", align_bytes=64)
-        in_planes_mid = sb.tile([P, PASSES, N], U8, name="in_planes_mid", align_bytes=64)
-        rest = sb.tile([P, W], F32, name="rest", align_bytes=64)
-        ea = sb.tile([P, PASSES, M], U32, name="ea", align_bytes=64)
+        ea_plane = sb.tile([P, PASSES, M], U8, name="in_planes_ea", align_bytes=64)
+        old_plane_first = sb.tile([P, PASSES, W], U8, name="in_planes_old0", align_bytes=64)
+        old_plane_rest = sb.tile([P, PASSES, N - W], U8, name="in_planes_old1", align_bytes=64)
+        mid_plane = sb.tile([P, PASSES, N], U8, name="in_planes_mid", align_bytes=64)
+        ea = tiles("ea", ROWS // FIRST, [P, PASSES, FIRST * P], U32)
         old = tiles("old", GROUPS, [P, PASSES, 2 * W], U8)
         mid = tiles("mid", GROUPS, [P, PASSES, W], U32)
         raw = tiles("raw", GROUPS * PASSES, [P, PACK, W], BF16)
-        scaled = tiles("scaled", 2, [P, PACK, W], BF16)
-        woven = tiles("woven", 2, [P, W, PACK], BF16)
+        scaled = tiles("scaled", PASSES, [P, PACK, W], BF16)
+        woven = tiles("woven", PASSES, [P, W, PACK], BF16)
         new = tiles("new", GROUPS * PASSES, [P, W], U32)
         new_plane = tiles("new_plane", GROUPS * PASSES, [P, W], U8)
-        b_sb = tiles("b_sb", GROUPS, [P, ROWS, W], BF16)
-        part = tiles("part", T_BUFS, [P, W], F32)
-        y = tiles("y", TILES, [P, W], F32)
-        y_bf = tiles("y_bf", YB_BUFS, [P, W], BF16)
-        y_t = tiles("y_t", 4, [P, 2 * P, PACK], BF16)
+        b_sb = tiles("b_sb", GROUPS, [P, ROWS * W], BF16)
+        acc = tiles("acc", PAIRS, [P, 2 * W], F32)
+        y_last = sb.tile([P, W], F32, name="y_last", align_bytes=64)
+        y_bf = tiles("y_bf", TILES, [P, W], BF16)
+        y_t = tiles("y_t", PAIRS, [P, 2 * P * PACK], BF16)
         out_words = tiles("out_words", GROUPS, [P, M], U32)
         out_plane = tiles("out_plane", GROUPS, [P, M], U8)
 
-        taken = []
+        free_banks = list(banks)
         bank_of = {}
 
         def take_bank(key):
-            bank_of[key] = banks[len(taken) % BANKS]
-            taken.append(key)
+            bank_of[key] = free_banks.pop(0)
             return bank_of[key]
+
+        def give_back(key):
+            free_banks.append(bank_of[key])
 
         def cols(g):
             return slice(g * W, (g + 1) * W)
+
+        def half(n):
+            return acc[n // 2][:, cols(n % 2)]
 
         ea_src = ea_words.rearrange("c p m t -> p c (m t)").bitcast(I32)
         old_src = old_words.rearrange("c p x -> p c x").bitcast(I32)
@@ -87,42 +89,46 @@ def tile_schur_window_block_k3_kernel(
         e_src = e_new.rearrange("(c p t) n -> c p t n", p=P, t=PACK)
         b_src = b.rearrange("(a p) n -> p a n", p=P)
 
-        def load_ea(a0, a1, queue=nc.sync):
-            queue.dma_start(out=ea[:, :, a0 * P : a1 * P].bitcast(I32), in_=ea_src[:, :, a0 * P : a1 * P])
+        def load_ea(i):
+            nc.sync.dma_start(out=ea[i][:].bitcast(I32), in_=ea_src[:, :, i * FIRST * P : (i + 1) * FIRST * P])
 
-        def load_old(g, queue=nc.sync):
-            queue.dma_start(out=old[g][:].bitcast(I32), in_=old_src[:, :, g * W // 2 : (g + 1) * W // 2])
+        def load_old(g):
+            nc.sync.dma_start(out=old[g][:].bitcast(I32), in_=old_src[:, :, g * W // 2 : (g + 1) * W // 2])
 
         def load_mid(g):
             nc.sync.dma_start(out=mid[g][:].bitcast(I32), in_=mid_src[:, :, cols(g)])
 
-        def load_e(g, c, queue=nc.sync):
-            queue.dma_start(out=raw[g * PASSES + c][:], in_=e_src[c][:, :, cols(g)])
+        def load_e(g, c):
+            nc.sync.dma_start(out=raw[g * PASSES + c][:], in_=e_src[c][:, :, cols(g)])
 
         def load_b(g, a0, a1):
-            nc.sync.dma_start(out=b_sb[g][:, a0:a1, :], in_=b_src[:, a0:a1, cols(g)])
+            dst = b_sb[g][:].rearrange("p (a n) -> p a n", n=W)
+            nc.sync.dma_start(out=dst[:, a0:a1, :], in_=b_src[:, a0:a1, cols(g)])
 
-        def load_plane(queue, plane, row0, scales, q0, q1, x0, x1):
+        def zero(plane):
+            nc.vector.memset(plane[:].rearrange("p c n -> p (c n)").bitcast(I32), 0)
+
+        def load_plane(plane, row0, scales):
             src = scales.rearrange("c q n -> q c n").bitcast(I32)
-            for quad in range(q0, q1):
+            for quad in range(4):
                 row = 32 * quad + row0
-                queue.dma_start(
-                    out=plane[row : row + 4, :, x0:x1].bitcast(I32), in_=src[4 * quad : 4 * quad + 4, :, x0 // 4 : x1 // 4]
-                )
+                nc.sync.dma_start(out=plane[row : row + 4, :, :].bitcast(I32), in_=src[4 * quad : 4 * quad + 4])
 
         def scale_rows(g, c):
-            s = g * PASSES + c
             for t in range(PACK):
                 k = c * PACK + t
                 nc.vector.tensor_scalar(
-                    out=scaled[s % 2][:, t, :], in0=raw[s][:, t, :], scalar1=d_inv[:, k : k + 1], scalar2=None, op0=ALU.mult
+                    out=scaled[c][:, t, :],
+                    in0=raw[g * PASSES + c][:, t, :],
+                    scalar1=d_inv[:, k : k + 1],
+                    scalar2=None,
+                    op0=ALU.mult,
                 )
 
-        def weave(g, c, half, engine):
-            s = g * PASSES + c
-            h = slice(half * W // 2, (half + 1) * W // 2)
-            dst = woven[s % 2][:, h, :].rearrange("p (c i) t -> p c t i", i=4)
-            src = scaled[s % 2][:, :, h].rearrange("p t (c i) -> p c t i", i=4)
+        def weave(c, h, engine):
+            part = slice(h * W // 2, (h + 1) * W // 2)
+            dst = woven[c][:, part, :].rearrange("p (x i) t -> p x t i", i=4)
+            src = scaled[c][:, :, part].rearrange("p t (x i) -> p x t i", i=4)
             if engine == "scalar":
                 nc.scalar.copy(out=dst, in_=src)
             else:
@@ -131,15 +137,15 @@ def tile_schur_window_block_k3_kernel(
         def quantize_new(g, c):
             s = g * PASSES + c
             nc.vector.quantize_mx(
-                out=new[s][:].bitcast(FP8X4), scales=new_plane[s][:], in_=woven[s % 2][:].rearrange("p w t -> p (w t)")
+                out=new[s][:].bitcast(FP8X4), scales=new_plane[s][:], in_=woven[c][:].rearrange("p w t -> p (w t)")
             )
 
         def mx(key, n, c, rhs, rhs_scale, start, stop):
             a = n % ROWS
             nc.tensor.matmul_mx(
                 out=bank_of[key][:],
-                lhsT=ea[:, c, a * P : (a + 1) * P].bitcast(FP8X4),
-                lhsT_scale=in_planes_ea[:, c, a * P : (a + 1) * P],
+                lhsT=ea[a // FIRST][:, c, a % FIRST * P : (a % FIRST + 1) * P].bitcast(FP8X4),
+                lhsT_scale=ea_plane[:, c, a * P : (a + 1) * P],
                 rhs=rhs,
                 rhs_scale=rhs_scale,
                 start=start,
@@ -150,78 +156,84 @@ def tile_schur_window_block_k3_kernel(
             g = n // ROWS
             take_bank(("old", n))
             for c in range(PASSES):
-                mx(("old", n), n, c, old[g][:, c, :].bitcast(FP4X4), in_planes_w[:, c, cols(g)], c == 0, c == PASSES - 1)
+                plane = old_plane_first[:, c, :] if g == 0 else old_plane_rest[:, c, cols(g - 1)]
+                mx(("old", n), n, c, old[g][:, c, :].bitcast(FP4X4), plane, c == 0, c == PASSES - 1)
 
         def mm_mid(n):
             g = n // ROWS
-            if n >= NEW_FIRST:
+            opens = n >= FIRST
+            if opens:
                 take_bank(("sum", n))
             for c in range(PASSES):
-                mx(("sum", n), n, c, mid[g][:, c, :].bitcast(FP8X4), in_planes_mid[MID_ROW:, c, cols(g)], c == 0 and n >= NEW_FIRST, False)
+                mx(("sum", n), n, c, mid[g][:, c, :].bitcast(FP8X4), mid_plane[MID_ROW:, c, cols(g)], opens and c == 0, False)
 
         def mm_new(n, c):
             s = n // ROWS * PASSES + c
-            opens = c == 0 and n < NEW_FIRST
+            opens = n < FIRST and c == 0
             if opens:
                 take_bank(("sum", n))
             mx(("sum", n), n, c, new[s][:].bitcast(FP8X4), new_plane[s][:], opens, c == PASSES - 1)
 
         def weigh_old(n):
-            nc.vector.tensor_tensor(
-                out=part[n % T_BUFS][:], in0=bank_of[("old", n)][:], in1=f_all[:, cols(n // ROWS)], op=ALU.mult
-            )
+            nc.vector.tensor_tensor(out=half(n), in0=bank_of[("old", n)][:], in1=f_all[:, cols(n // ROWS)], op=ALU.mult)
+            give_back(("old", n))
 
-        def remainder(n):
-            return rest if ON_G(n) else part[n % T_BUFS]
-
-        def from_b(n):
-            eng = nc.gpsimd if ON_G(n) else nc.vector
+        def from_b(q, x0, x1, engine):
+            g, at = 2 * q // ROWS, 2 * q % ROWS * W
+            eng = nc.gpsimd if engine == "gpsimd" else nc.vector
             eng.tensor_tensor(
-                out=remainder(n)[:], in0=b_sb[n // ROWS][:, n % ROWS, :], in1=part[n % T_BUFS][:], op=ALU.subtract
+                out=acc[q][:, x0:x1], in0=b_sb[g][:, at + x0 : at + x1], in1=acc[q][:, x0:x1], op=ALU.subtract
             )
 
         def finish(n):
-            nc.vector.tensor_tensor(out=y[n][:], in0=remainder(n)[:], in1=bank_of[("sum", n)][:], op=ALU.subtract)
+            out = y_last[:] if n == TILES - 1 else half(n)
+            nc.vector.tensor_tensor(out=out, in0=half(n), in1=bank_of[("sum", n)][:], op=ALU.subtract)
+            give_back(("sum", n))
 
         def round_y(n):
             nc.scalar.copy(
-                out=y_bf[n % YB_BUFS][:].rearrange("p (u j e) -> p u j e", u=2, e=2),
-                in_=y[n][:].rearrange("p (j u e) -> p u j e", u=2, e=2),
+                out=y_bf[n][:].rearrange("p (u j e) -> p u j e", u=2, e=2),
+                in_=half(n).rearrange("p (j u e) -> p u j e", u=2, e=2),
+            )
+
+        def round_last(n):
+            nc.vector.tensor_tensor(
+                out=y_bf[n][:].rearrange("p (u j e) -> p u j e", u=2, e=2),
+                in0=half(n).rearrange("p (j u e) -> p u j e", u=2, e=2),
+                in1=bank_of[("sum", n)][:].rearrange("p (j u e) -> p u j e", u=2, e=2),
+                op=ALU.subtract,
             )
 
         def turn(n0, count):
             bank = take_bank(("turn", n0))
             for h in range(count):
-                words = y_bf[(n0 + h) % YB_BUFS][:].bitcast(F32)
+                words = y_bf[n0 + h][:].bitcast(F32)
                 for u in range(2):
                     o = (count * u + h) * P
                     nc.tensor.transpose(bank[:, o : o + P], words[:, u * P : (u + 1) * P], ident[:])
 
         def copy_turned(n0, count):
+            at = n0 % 2 * W
             nc.scalar.copy(
-                out=y_t[(n0 + 1) // 2 % 4][:, : count * P, :].rearrange("p m t -> p (m t)").bitcast(F32).rearrange("p (m u) -> p m u", u=2),
+                out=y_t[n0 // 2][:, at : at + count * W].bitcast(F32).rearrange("p (m u) -> p m u", u=2),
                 in_=bank_of[("turn", n0)][:, : 2 * count * P].rearrange("p (u m) -> p m u", u=2),
             )
+            give_back(("turn", n0))
 
         def quantize_y(n0, count):
-            g, m0 = n0 // ROWS, n0 % ROWS * P
+            g, m0, at = n0 // ROWS, n0 % ROWS * P, n0 % 2 * W
             nc.vector.quantize_mx(
                 out=out_words[g][:, m0 : m0 + count * P].bitcast(FP8X4),
                 scales=out_plane[g][:, m0 : m0 + count * P],
-                in_=y_t[(n0 + 1) // 2 % 4][:, : count * P, :].rearrange("p m t -> p (m t)"),
+                in_=y_t[n0 // 2][:, at : at + count * W],
             )
 
-        def round_last(n):
-            nc.vector.tensor_tensor(
-                out=y_bf[n % YB_BUFS][:].rearrange("p (u j e) -> p u j e", u=2, e=2),
-                in0=remainder(n)[:].rearrange("p (j u e) -> p u j e", u=2, e=2),
-                in1=bank_of[("sum", n)][:].rearrange("p (j u e) -> p u j e", u=2, e=2),
-                op=ALU.subtract,
-            )
-
-        def store_y(n):
-            a = n % ROWS
-            nc.sync.dma_start(out=out_0[a * P : (a + 1) * P, cols(n // ROWS)], in_=y[n][:])
+        def store_y(n0, count):
+            a = n0 % ROWS
+            dst = out_0[a * P : (a + count) * P, cols(n0 // ROWS)].rearrange("(h p) n -> p h n", p=P)
+            at = n0 % 2 * W
+            src = y_last[:] if n0 == TILES - 1 else acc[n0 // 2][:, at : at + count * W]
+            nc.sync.dma_start(out=dst, in_=src.rearrange("p (h n) -> p h n", n=W))
 
         def store_words(g, m0, m1):
             dst = out_1[g].rearrange("p m t -> p (m t)").bitcast(I32)
@@ -234,28 +246,28 @@ def tile_schur_window_block_k3_kernel(
                     in_=out_plane[g][32 * quad : 32 * quad + 4, :].bitcast(I32),
                 )
 
-
-        nc.vector.memset(in_planes_ea[:].rearrange("p c m -> p (c m)").bitcast(I32), 0)
-        nc.vector.memset(in_planes_w[:].rearrange("p c n -> p (c n)").bitcast(I32), 0)
+        zero(ea_plane)
+        zero(old_plane_first)
         make_identity(nc, ident[:])
+        zero(mid_plane)
+        zero(old_plane_rest)
         nc.sync.dma_start(out=d_sb[:], in_=d.rearrange("(c p t) -> p c t", p=P, t=PACK))
         nc.sync.dma_start(out=f_sb[:], in_=f.rearrange("(g p t) -> p g t", p=P, t=PACK))
-        nc.vector.memset(in_planes_mid[:].rearrange("p c n -> p (c n)").bitcast(I32), 0)
         load_e(0, 0)
-        load_plane(nc.sync, in_planes_ea, 0, ea_scales, 0, 4, 0, M)
-        load_ea(0, EA_FIRST)
+        load_plane(ea_plane, 0, ea_scales)
+        load_ea(0)
         load_old(0)
-        load_plane(nc.sync, in_planes_w, 0, old_scales, 0, 4, 0, W)
+        load_plane(old_plane_first, 0, old_scales[:, :, :W])
         load_e(0, 1)
         load_mid(0)
-        load_plane(nc.sync, in_planes_mid, MID_ROW, mid_scales, 0, 4, 0, N)
+        load_plane(mid_plane, MID_ROW, mid_scales)
         load_b(0, 0, 2)
-        load_ea(EA_FIRST, ROWS)
+        load_ea(1)
         load_e(1, 0)
-        load_plane(nc.sync, in_planes_w, 0, old_scales, 0, 4, W, N)
+        load_plane(old_plane_rest, 0, old_scales[:, :, W:])
+        load_old(1)
         load_b(0, 2, ROWS)
         load_e(1, 1)
-        load_old(1)
         load_mid(1)
         load_b(1, 0, ROWS)
         load_e(2, 0)
@@ -277,99 +289,108 @@ def tile_schur_window_block_k3_kernel(
                 out=f_all[:, cols(g)].bitcast(F32).rearrange("p (j u) -> p j u", u=2),
                 in_=f_banks[g // 2][:, o : o + 2 * P].rearrange("p (u j) -> p j u", u=2),
             )
+            if g > 0:
+                give_back(("f", g // 2))
 
         spread_f(0)
         mm_old(0)
         mm_old(1)
+        mm_old(2)
         scale_rows(0, 0)
-        weave(0, 0, 0, "scalar")
-        weave(0, 0, 1, "vector")
+        weave(0, 0, "scalar")
+        weave(0, 1, "vector")
         spread_f(1)
         spread_f(2)
         quantize_new(0, 0)
-        for n in range(NEW_FIRST):
+        for n in range(FIRST):
             mm_new(n, 0)
-        mm_old(2)
         scale_rows(0, 1)
-        weave(0, 1, 0, "scalar")
+        weave(1, 0, "scalar")
         weigh_old(0)
-        weave(0, 1, 1, "vector")
-        for n in range(NEW_FIRST):
+        weave(1, 1, "vector")
+        for n in range(FIRST):
             mm_mid(n)
         weigh_old(1)
-        from_b(0)
+        from_b(0, 0, W, "vector")
         quantize_new(0, 1)
         weigh_old(2)
-        from_b(2)
-
-        TURN = {2: [0], 8: [2, 4, 6], 12: [8, 10], 14: [12]}
         scale_rows(1, 0)
-        for a in range(0, TILES, 2):
-            g, k = a // ROWS + 1, a % ROWS // 2
+
+        TURN = {1: [0], 4: [1, 2, 3], 6: [4, 5], 7: [6]}
+        for q in range(PAIRS):
+            a = 2 * q
+            g, k = a // ROWS + 1, q % (ROWS // 2)
             prep = g < GROUPS
-            last = a == TILES - 2
-            due = TURN.get(a - 2, [])
+            last = q == PAIRS - 1
+            due = TURN.get(q - 1, [])
             for n in (a, a + 1):
-                if n >= NEW_FIRST:
+                if n + 3 < TILES - 1:
+                    mm_old(n + 3)
+                if n >= FIRST:
                     mm_mid(n)
                     mm_new(n, 0)
                 if n == TILES - 1:
                     turn(a - 2, 2)
                 mm_new(n, 1)
-                if n == a:
-                    for m in (a + 3, a + 4):
-                        if m < TILES:
-                            mm_old(m)
-            for q in TURN.get(a, []):
-                turn(q, 2)
+            if q == PAIRS - 3:
+                mm_old(TILES - 1)
+            for r in TURN.get(q, []):
+                turn(2 * r, 2)
             if prep and k < PASSES:
-                weave(g, k, 0, "scalar")
-            for q in due:
-                copy_turned(q, 2)
-            finish(a)
-            if 0 < a < TILES - 2:
-                from_b(a + 2)
+                weave(k, 0, "scalar")
+                weave(k, 1, "scalar")
+            for r in due:
+                copy_turned(2 * r, 2)
+            if q < PAIRS - 2:
+                weigh_old(a + 3)
+                from_b(q + 1, 0, POOL_COLS, "gpsimd")
             if not last:
-                from_b(a + 1)
-            else:
-                for q in due:
-                    quantize_y(q, 2)
-                copy_turned(a - 2, 2)
+                from_b(q, POOL_COLS if q > 0 else W, 2 * W, "vector")
+            finish(a)
+            if last:
+                for r in due:
+                    quantize_y(2 * r, 2)
+                store_words(GROUPS - 1, 0, 2 * P)
             round_y(a)
-            if prep and k < PASSES:
-                weave(g, k, 1, "scalar")
-            for m in (a + 3, a + 4):
-                if m < TILES:
-                    weigh_old(m)
+            if last:
+                copy_turned(a - 2, 2)
+            if a + 4 < TILES:
+                weigh_old(a + 4)
             if last:
                 round_last(a + 1)
             finish(a + 1)
             if not last:
                 round_y(a + 1)
-            if a == TILES - 4:
-                from_b(TILES - 1)
+            if q == PAIRS - 2:
+                from_b(q + 1, POOL_COLS, 2 * W, "vector")
             if prep and k == 0:
                 scale_rows(g, 1)
             if g + 1 < GROUPS and k == 2:
                 scale_rows(g + 1, 0)
             if not last:
-                for q in due:
-                    quantize_y(q, 2)
+                for r in due:
+                    quantize_y(2 * r, 2)
             if prep and k < PASSES:
                 quantize_new(g, k)
-            store_y(a)
-            store_y(a + 1)
-            for q in due:
-                if q % ROWS == ROWS - 2:
-                    store_words(q // ROWS, 0, M)
-                    store_plane(q // ROWS, [nc.sync] * 4)
+            if q == PAIRS - 3:
+                weigh_old(TILES - 1)
+                from_b(PAIRS - 1, 0, POOL_COLS, "gpsimd")
+            if last:
+                store_y(a, 1)
+                store_y(a + 1, 1)
+            else:
+                store_y(a, 2)
+            for r in due:
+                if r % 3 == 2:
+                    store_words(r // 3, 0, M)
+                    store_plane(r // 3, [nc.sync] * 4)
         turn(16, 1)
         turn(17, 1)
-        quantize_y(14, 2)
-        store_words(2, 0, 4 * P)
         copy_turned(16, 1)
         copy_turned(17, 1)
+        quantize_y(14, 2)
         quantize_y(16, 1)
+        store_words(2, 2 * P, 5 * P)
         quantize_y(17, 1)
-        store_words(2, 4 * P, 6 * P)
+        store_words(2, 5 * P, 6 * P)
         store_plane(2, [nc.scalar, nc.sync, nc.scalar, nc.sync])

@@ -26,7 +26,7 @@ PAIRS = TILES // 2
 BANKS = 8
 FIRST = 3
 MID_ROW = 4
-POOL_COLS = 640
+SPLIT = 512
 
 
 def tile_schur_window_block_k3_kernel(
@@ -246,13 +246,13 @@ def tile_schur_window_block_k3_kernel(
                     in_=out_plane[g][32 * quad : 32 * quad + 4, :].bitcast(I32),
                 )
 
+        nc.gpsimd.dma_start(out=f_sb[:], in_=f.rearrange("(g p t) -> p g t", p=P, t=PACK))
+        nc.sync.dma_start(out=d_sb[:], in_=d.rearrange("(c p t) -> p c t", p=P, t=PACK))
         zero(ea_plane)
         zero(old_plane_first)
         make_identity(nc, ident[:])
         zero(mid_plane)
         zero(old_plane_rest)
-        nc.sync.dma_start(out=d_sb[:], in_=d.rearrange("(c p t) -> p c t", p=P, t=PACK))
-        nc.sync.dma_start(out=f_sb[:], in_=f.rearrange("(g p t) -> p g t", p=P, t=PACK))
         load_e(0, 0)
         load_plane(ea_plane, 0, ea_scales)
         load_ea(0)
@@ -343,9 +343,11 @@ def tile_schur_window_block_k3_kernel(
                 copy_turned(2 * r, 2)
             if q < PAIRS - 2:
                 weigh_old(a + 3)
-                from_b(q + 1, 0, POOL_COLS, "gpsimd")
+                from_b(q + 1, SPLIT, 2 * W, "gpsimd")
             if not last:
-                from_b(q, POOL_COLS if q > 0 else W, 2 * W, "vector")
+                from_b(q, 0 if q > 0 else W, SPLIT if q > 0 else 2 * W, "vector")
+            if a + 4 < TILES:
+                weigh_old(a + 4)
             finish(a)
             if last:
                 for r in due:
@@ -354,15 +356,13 @@ def tile_schur_window_block_k3_kernel(
             round_y(a)
             if last:
                 copy_turned(a - 2, 2)
-            if a + 4 < TILES:
-                weigh_old(a + 4)
             if last:
                 round_last(a + 1)
             finish(a + 1)
             if not last:
                 round_y(a + 1)
             if q == PAIRS - 2:
-                from_b(q + 1, POOL_COLS, 2 * W, "vector")
+                from_b(q + 1, 0, SPLIT, "vector")
             if prep and k == 0:
                 scale_rows(g, 1)
             if g + 1 < GROUPS and k == 2:
@@ -374,7 +374,7 @@ def tile_schur_window_block_k3_kernel(
                 quantize_new(g, k)
             if q == PAIRS - 3:
                 weigh_old(TILES - 1)
-                from_b(PAIRS - 1, 0, POOL_COLS, "gpsimd")
+                from_b(PAIRS - 1, SPLIT, 2 * W, "gpsimd")
             if last:
                 store_y(a, 1)
                 store_y(a + 1, 1)
@@ -390,7 +390,6 @@ def tile_schur_window_block_k3_kernel(
         copy_turned(17, 1)
         quantize_y(14, 2)
         quantize_y(16, 1)
-        store_words(2, 2 * P, 5 * P)
         quantize_y(17, 1)
-        store_words(2, 5 * P, 6 * P)
+        store_words(2, 2 * P, 6 * P)
         store_plane(2, [nc.scalar, nc.sync, nc.scalar, nc.sync])

@@ -14,6 +14,7 @@ U8 = mybir.dt.uint8
 FP8X4 = mybir.dt.float8_e4m3fn_x4
 FP4X4 = mybir.dt.float4_e2m1fn_x4
 ALU = mybir.AluOpType
+ACT = mybir.ActivationFunctionType
 
 P = 128
 PACK = 4
@@ -26,7 +27,8 @@ PAIRS = TILES // 2
 BANKS = 8
 FIRST = 3
 MID_ROW = 4
-SPLIT = 512
+WARM_PASSES = 6
+SPLIT = 384
 
 
 def tile_schur_window_block_k3_kernel(
@@ -39,18 +41,18 @@ def tile_schur_window_block_k3_kernel(
         ctx.enter_context(tc.manual_schedule())
 
         def tiles(name, count, shape, dtype):
-            return [sb.tile(shape, dtype, name="%s%d" % (name, i), align_bytes=64) for i in range(count)]
+            return [sb.tile(shape, dtype, name="%s%d" % (name, i), align_bytes=256) for i in range(count)]
 
         banks = [ps.tile([P, W], F32, name="bank%d" % i) for i in range(BANKS)]
-        ident = sb.tile([P, P], F32, name="ident", align_bytes=64)
-        d_sb = sb.tile([P, PASSES, PACK], BF16, name="d_sb", align_bytes=64)
-        d_inv = sb.tile([P, PASSES * PACK], F32, name="d_inv", align_bytes=64)
-        f_sb = sb.tile([P, GROUPS, PACK], BF16, name="f_sb", align_bytes=64)
-        f_all = sb.tile([P, N], BF16, name="f_all", align_bytes=64)
-        ea_plane = sb.tile([P, PASSES, M], U8, name="in_planes_ea", align_bytes=64)
-        old_plane_first = sb.tile([P, PASSES, W], U8, name="in_planes_old0", align_bytes=64)
-        old_plane_rest = sb.tile([P, PASSES, N - W], U8, name="in_planes_old1", align_bytes=64)
-        mid_plane = sb.tile([P, PASSES, N], U8, name="in_planes_mid", align_bytes=64)
+        ident = sb.tile([P, P], F32, name="ident", align_bytes=256)
+        d_sb = sb.tile([P, PASSES, PACK], BF16, name="d_sb", align_bytes=256)
+        d_inv = sb.tile([P, PASSES * PACK], F32, name="d_inv", align_bytes=256)
+        f_sb = sb.tile([P, GROUPS, PACK], BF16, name="f_sb", align_bytes=256)
+        f_all = sb.tile([P, N], BF16, name="f_all", align_bytes=256)
+        ea_plane = sb.tile([P, PASSES, M], U8, name="in_planes_ea", align_bytes=256)
+        old_plane_first = sb.tile([P, PASSES, W], U8, name="in_planes_old0", align_bytes=256)
+        old_plane_rest = sb.tile([P, PASSES, N - W], U8, name="in_planes_old1", align_bytes=256)
+        mid_plane = sb.tile([P, PASSES, N], U8, name="in_planes_mid", align_bytes=256)
         ea = tiles("ea", ROWS // FIRST, [P, PASSES, FIRST * P], U32)
         old = tiles("old", GROUPS, [P, PASSES, 2 * W], U8)
         mid = tiles("mid", GROUPS, [P, PASSES, W], U32)
@@ -61,7 +63,7 @@ def tile_schur_window_block_k3_kernel(
         new_plane = tiles("new_plane", GROUPS * PASSES, [P, W], U8)
         b_sb = tiles("b_sb", GROUPS, [P, ROWS * W], BF16)
         acc = tiles("acc", PAIRS, [P, 2 * W], F32)
-        y_last = sb.tile([P, W], F32, name="y_last", align_bytes=64)
+        y_last = sb.tile([P, W], F32, name="y_last", align_bytes=256)
         y_bf = tiles("y_bf", TILES, [P, W], BF16)
         y_t = tiles("y_t", PAIRS, [P, 2 * P * PACK], BF16)
         out_words = tiles("out_words", GROUPS, [P, M], U32)
@@ -114,16 +116,14 @@ def tile_schur_window_block_k3_kernel(
                 row = 32 * quad + row0
                 nc.sync.dma_start(out=plane[row : row + 4, :, :].bitcast(I32), in_=src[4 * quad : 4 * quad + 4])
 
-        def scale_rows(g, c):
+        def scale_rows(g, c, engine):
             for t in range(PACK):
-                k = c * PACK + t
-                nc.vector.tensor_scalar(
-                    out=scaled[c][:, t, :],
-                    in0=raw[g * PASSES + c][:, t, :],
-                    scalar1=d_inv[:, k : k + 1],
-                    scalar2=None,
-                    op0=ALU.mult,
-                )
+                dst, src = scaled[c][:, t, :], raw[g * PASSES + c][:, t, :]
+                factor = d_inv[:, c * PACK + t : c * PACK + t + 1]
+                if engine == "scalar":
+                    nc.scalar.activation(out=dst, in_=src, func=ACT.Copy, scale=factor)
+                else:
+                    nc.vector.tensor_scalar(out=dst, in0=src, scalar1=factor, scalar2=None, op0=ALU.mult)
 
         def weave(c, h, engine):
             part = slice(h * W // 2, (h + 1) * W // 2)
@@ -159,13 +159,12 @@ def tile_schur_window_block_k3_kernel(
                 plane = old_plane_first[:, c, :] if g == 0 else old_plane_rest[:, c, cols(g - 1)]
                 mx(("old", n), n, c, old[g][:, c, :].bitcast(FP4X4), plane, c == 0, c == PASSES - 1)
 
-        def mm_mid(n):
+        def mm_mid(n, c):
             g = n // ROWS
-            opens = n >= FIRST
+            opens = n >= FIRST and c == 0
             if opens:
                 take_bank(("sum", n))
-            for c in range(PASSES):
-                mx(("sum", n), n, c, mid[g][:, c, :].bitcast(FP8X4), mid_plane[MID_ROW:, c, cols(g)], opens and c == 0, False)
+            mx(("sum", n), n, c, mid[g][:, c, :].bitcast(FP8X4), mid_plane[MID_ROW:, c, cols(g)], opens, False)
 
         def mm_new(n, c):
             s = n // ROWS * PASSES + c
@@ -246,28 +245,29 @@ def tile_schur_window_block_k3_kernel(
                     in_=out_plane[g][32 * quad : 32 * quad + 4, :].bitcast(I32),
                 )
 
-        nc.gpsimd.dma_start(out=f_sb[:], in_=f.rearrange("(g p t) -> p g t", p=P, t=PACK))
         nc.sync.dma_start(out=d_sb[:], in_=d.rearrange("(c p t) -> p c t", p=P, t=PACK))
+        nc.sync.dma_start(out=f_sb[:], in_=f.rearrange("(g p t) -> p g t", p=P, t=PACK))
         zero(ea_plane)
         zero(old_plane_first)
         make_identity(nc, ident[:])
         zero(mid_plane)
         zero(old_plane_rest)
-        load_e(0, 0)
-        load_plane(ea_plane, 0, ea_scales)
         load_ea(0)
+        load_plane(ea_plane, 0, ea_scales)
+        load_e(0, 0)
         load_old(0)
         load_plane(old_plane_first, 0, old_scales[:, :, :W])
         load_e(0, 1)
+        load_ea(1)
         load_mid(0)
         load_plane(mid_plane, MID_ROW, mid_scales)
         load_b(0, 0, 2)
-        load_ea(1)
         load_e(1, 0)
+        load_b(0, 2, 4)
         load_plane(old_plane_rest, 0, old_scales[:, :, W:])
         load_old(1)
-        load_b(0, 2, ROWS)
         load_e(1, 1)
+        load_b(0, 4, 6)
         load_mid(1)
         load_b(1, 0, ROWS)
         load_e(2, 0)
@@ -292,50 +292,64 @@ def tile_schur_window_block_k3_kernel(
             if g > 0:
                 give_back(("f", g // 2))
 
-        spread_f(0)
-        mm_old(0)
-        mm_old(1)
-        mm_old(2)
-        scale_rows(0, 0)
+        warm = take_bank("warm")
+        give_back("warm")
+        for i in range(WARM_PASSES):
+            nc.tensor.matmul_mx(
+                out=warm[:, : 2 * P],
+                lhsT=ea[0][:, 0, :P].bitcast(FP8X4),
+                lhsT_scale=ea_plane[:, 0, :P],
+                rhs=ea[0][:, 0, : 2 * P].bitcast(FP8X4),
+                rhs_scale=ea_plane[:, 0, : 2 * P],
+                start=True,
+                stop=True,
+            )
+        for g in range(GROUPS):
+            spread_f(g)
+        for n in range(FIRST):
+            mm_old(n)
+        scale_rows(0, 0, "vector")
         weave(0, 0, "scalar")
         weave(0, 1, "vector")
-        spread_f(1)
-        spread_f(2)
+        scale_rows(0, 1, "vector")
         quantize_new(0, 0)
+        weave(1, 0, "scalar")
+        weave(1, 1, "scalar")
+        mm_old(FIRST)
         for n in range(FIRST):
             mm_new(n, 0)
-        scale_rows(0, 1)
-        weave(1, 0, "scalar")
-        weigh_old(0)
-        weave(1, 1, "vector")
         for n in range(FIRST):
-            mm_mid(n)
-        weigh_old(1)
-        from_b(0, 0, W, "vector")
+            weigh_old(n)
+        for n in range(FIRST + 1, ROWS):
+            mm_old(n)
+        for n in range(FIRST):
+            mm_mid(n, 0)
+            mm_mid(n, 1)
+        from_b(0, 0, 2 * W, "vector")
         quantize_new(0, 1)
-        weigh_old(2)
-        scale_rows(1, 0)
+        scale_rows(1, 0, "vector")
 
-        TURN = {1: [0], 4: [1, 2, 3], 6: [4, 5], 7: [6]}
+        TURN = {4: [0], 10: [1, 2], 13: [3, 4, 5], 15: [6]}
         for q in range(PAIRS):
             a = 2 * q
             g, k = a // ROWS + 1, q % (ROWS // 2)
             prep = g < GROUPS
             last = q == PAIRS - 1
-            due = TURN.get(q - 1, [])
+            due = TURN.get(a - 1, []) + TURN.get(a, [])
             for n in (a, a + 1):
-                if n + 3 < TILES - 1:
+                if ROWS <= n + 3 < TILES - 1:
                     mm_old(n + 3)
                 if n >= FIRST:
-                    mm_mid(n)
+                    mm_mid(n, 0)
                     mm_new(n, 0)
+                    mm_mid(n, 1)
                 if n == TILES - 1:
                     turn(a - 2, 2)
                 mm_new(n, 1)
+                for r in TURN.get(n, []):
+                    turn(2 * r, 2)
             if q == PAIRS - 3:
                 mm_old(TILES - 1)
-            for r in TURN.get(q, []):
-                turn(2 * r, 2)
             if prep and k < PASSES:
                 weave(k, 0, "scalar")
                 weave(k, 1, "scalar")
@@ -344,8 +358,8 @@ def tile_schur_window_block_k3_kernel(
             if q < PAIRS - 2:
                 weigh_old(a + 3)
                 from_b(q + 1, SPLIT, 2 * W, "gpsimd")
-            if not last:
-                from_b(q, 0 if q > 0 else W, SPLIT if q > 0 else 2 * W, "vector")
+            if 0 < q < PAIRS - 1:
+                from_b(q, 0, SPLIT, "vector")
             if a + 4 < TILES:
                 weigh_old(a + 4)
             finish(a)
@@ -364,9 +378,9 @@ def tile_schur_window_block_k3_kernel(
             if q == PAIRS - 2:
                 from_b(q + 1, 0, SPLIT, "vector")
             if prep and k == 0:
-                scale_rows(g, 1)
+                scale_rows(g, 1, "vector")
             if g + 1 < GROUPS and k == 2:
-                scale_rows(g + 1, 0)
+                scale_rows(g + 1, 0, "vector")
             if not last:
                 for r in due:
                     quantize_y(2 * r, 2)

@@ -14,7 +14,6 @@ U8 = mybir.dt.uint8
 FP8X4 = mybir.dt.float8_e4m3fn_x4
 FP4X4 = mybir.dt.float4_e2m1fn_x4
 ALU = mybir.AluOpType
-ACT = mybir.ActivationFunctionType
 
 P = 128
 PACK = 4
@@ -24,11 +23,16 @@ GROUPS = N // W
 ROWS = M // P
 TILES = GROUPS * ROWS
 PAIRS = TILES // 2
+PAIRS_IN_GROUP = ROWS // 2
 BANKS = 8
+ALIGN = 256
 FIRST = 3
+LEAD = 3
 MID_ROW = 4
+QUADS = (0, 2, 1, 3)
 WARM_PASSES = 6
-SPLIT = 384
+SPLIT = 352
+TURN_AFTER = {4: [0], 10: [1, 2], 13: [3, 4, 5], 15: [6]}
 
 
 def tile_schur_window_block_k3_kernel(
@@ -40,19 +44,23 @@ def tile_schur_window_block_k3_kernel(
         ps = ctx.enter_context(tc.psum_pool(name="ps", bufs=1))
         ctx.enter_context(tc.manual_schedule())
 
+        def tile(name, shape, dtype):
+            return sb.tile(shape, dtype, name=name, align_bytes=ALIGN)
+
         def tiles(name, count, shape, dtype):
-            return [sb.tile(shape, dtype, name="%s%d" % (name, i), align_bytes=256) for i in range(count)]
+            return [tile("%s%d" % (name, i), shape, dtype) for i in range(count)]
 
         banks = [ps.tile([P, W], F32, name="bank%d" % i) for i in range(BANKS)]
-        ident = sb.tile([P, P], F32, name="ident", align_bytes=256)
-        d_sb = sb.tile([P, PASSES, PACK], BF16, name="d_sb", align_bytes=256)
-        d_inv = sb.tile([P, PASSES * PACK], F32, name="d_inv", align_bytes=256)
-        f_sb = sb.tile([P, GROUPS, PACK], BF16, name="f_sb", align_bytes=256)
-        f_all = sb.tile([P, N], BF16, name="f_all", align_bytes=256)
-        ea_plane = sb.tile([P, PASSES, M], U8, name="in_planes_ea", align_bytes=256)
-        old_plane_first = sb.tile([P, PASSES, W], U8, name="in_planes_old0", align_bytes=256)
-        old_plane_rest = sb.tile([P, PASSES, N - W], U8, name="in_planes_old1", align_bytes=256)
-        mid_plane = sb.tile([P, PASSES, N], U8, name="in_planes_mid", align_bytes=256)
+        ident = tile("ident", [P, P], F32)
+        d_sb = tile("d_sb", [P, PASSES, PACK], BF16)
+        d_inv = tile("d_inv", [P, PASSES * PACK], F32)
+        f_sb = tile("f_sb", [P, GROUPS, PACK], BF16)
+        f_all = tile("f_all", [P, N], BF16)
+        ea_plane = tile("ea_plane", [P, PASSES, M], U8)
+        old_plane_first = tile("old_plane_first", [P, PASSES, W], U8)
+        old_plane_rest = tile("old_plane_rest", [P, PASSES, N - W], U8)
+        mid_plane_first = tile("mid_plane_first", [P, PASSES, W], U8)
+        mid_plane_rest = tile("mid_plane_rest", [P, PASSES, N - W], U8)
         ea = tiles("ea", ROWS // FIRST, [P, PASSES, FIRST * P], U32)
         old = tiles("old", GROUPS, [P, PASSES, 2 * W], U8)
         mid = tiles("mid", GROUPS, [P, PASSES, W], U32)
@@ -63,9 +71,9 @@ def tile_schur_window_block_k3_kernel(
         new_plane = tiles("new_plane", GROUPS * PASSES, [P, W], U8)
         b_sb = tiles("b_sb", GROUPS, [P, ROWS * W], BF16)
         acc = tiles("acc", PAIRS, [P, 2 * W], F32)
-        y_last = sb.tile([P, W], F32, name="y_last", align_bytes=256)
+        y_last = tile("y_last", [P, W], F32)
         y_bf = tiles("y_bf", TILES, [P, W], BF16)
-        y_t = tiles("y_t", PAIRS, [P, 2 * P * PACK], BF16)
+        y_t = tiles("y_t", GROUPS, [P, M * PACK], BF16)
         out_words = tiles("out_words", GROUPS, [P, M], U32)
         out_plane = tiles("out_plane", GROUPS, [P, M], U8)
 
@@ -79,10 +87,10 @@ def tile_schur_window_block_k3_kernel(
         def give_back(key):
             free_banks.append(bank_of[key])
 
-        def cols(g):
-            return slice(g * W, (g + 1) * W)
+        def cols(index):
+            return slice(index * W, (index + 1) * W)
 
-        def half(n):
+        def acc_of(n):
             return acc[n // 2][:, cols(n % 2)]
 
         ea_src = ea_words.rearrange("c p m t -> p c (m t)").bitcast(I32)
@@ -91,8 +99,9 @@ def tile_schur_window_block_k3_kernel(
         e_src = e_new.rearrange("(c p t) n -> c p t n", p=P, t=PACK)
         b_src = b.rearrange("(a p) n -> p a n", p=P)
 
-        def load_ea(i):
-            nc.sync.dma_start(out=ea[i][:].bitcast(I32), in_=ea_src[:, :, i * FIRST * P : (i + 1) * FIRST * P])
+        def load_ea(part):
+            span = slice(part * FIRST * P, (part + 1) * FIRST * P)
+            nc.sync.dma_start(out=ea[part][:].bitcast(I32), in_=ea_src[:, :, span])
 
         def load_old(g):
             nc.sync.dma_start(out=old[g][:].bitcast(I32), in_=old_src[:, :, g * W // 2 : (g + 1) * W // 2])
@@ -103,60 +112,62 @@ def tile_schur_window_block_k3_kernel(
         def load_e(g, c):
             nc.sync.dma_start(out=raw[g * PASSES + c][:], in_=e_src[c][:, :, cols(g)])
 
-        def load_b(g, a0, a1):
+        def load_b(g, block0, block1):
             dst = b_sb[g][:].rearrange("p (a n) -> p a n", n=W)
-            nc.sync.dma_start(out=dst[:, a0:a1, :], in_=b_src[:, a0:a1, cols(g)])
+            nc.sync.dma_start(out=dst[:, block0:block1, :], in_=b_src[:, block0:block1, cols(g)])
 
         def zero(plane):
             nc.vector.memset(plane[:].rearrange("p c n -> p (c n)").bitcast(I32), 0)
 
         def load_plane(plane, row0, scales):
             src = scales.rearrange("c q n -> q c n").bitcast(I32)
-            for quad in range(4):
+            for quad in QUADS:
                 row = 32 * quad + row0
                 nc.sync.dma_start(out=plane[row : row + 4, :, :].bitcast(I32), in_=src[4 * quad : 4 * quad + 4])
 
-        def scale_rows(g, c, engine):
+        def scale_rows(g, c):
             for t in range(PACK):
-                dst, src = scaled[c][:, t, :], raw[g * PASSES + c][:, t, :]
-                factor = d_inv[:, c * PACK + t : c * PACK + t + 1]
-                if engine == "scalar":
-                    nc.scalar.activation(out=dst, in_=src, func=ACT.Copy, scale=factor)
-                else:
-                    nc.vector.tensor_scalar(out=dst, in0=src, scalar1=factor, scalar2=None, op0=ALU.mult)
+                nc.vector.tensor_scalar(
+                    out=scaled[c][:, t, :],
+                    in0=raw[g * PASSES + c][:, t, :],
+                    scalar1=d_inv[:, c * PACK + t : c * PACK + t + 1],
+                    scalar2=None,
+                    op0=ALU.mult,
+                )
 
-        def weave(c, h, engine):
-            part = slice(h * W // 2, (h + 1) * W // 2)
-            dst = woven[c][:, part, :].rearrange("p (x i) t -> p x t i", i=4)
-            src = scaled[c][:, :, part].rearrange("p t (x i) -> p x t i", i=4)
-            if engine == "scalar":
-                nc.scalar.copy(out=dst, in_=src)
-            else:
-                nc.vector.tensor_copy(out=dst, in_=src)
+        def weave(c, col0, col1, copy):
+            copy(
+                out=woven[c][:, col0:col1, :].rearrange("p (x i) t -> p x t i", i=4),
+                in_=scaled[c][:, :, col0:col1].rearrange("p t (x i) -> p x t i", i=4),
+            )
 
         def quantize_new(g, c):
-            s = g * PASSES + c
             nc.vector.quantize_mx(
-                out=new[s][:].bitcast(FP8X4), scales=new_plane[s][:], in_=woven[c][:].rearrange("p w t -> p (w t)")
+                out=new[g * PASSES + c][:].bitcast(FP8X4),
+                scales=new_plane[g * PASSES + c][:],
+                in_=woven[c][:].rearrange("p w t -> p (w t)"),
             )
 
         def mx(key, n, c, rhs, rhs_scale, start, stop):
-            a = n % ROWS
+            block = n % ROWS
             nc.tensor.matmul_mx(
                 out=bank_of[key][:],
-                lhsT=ea[a // FIRST][:, c, a % FIRST * P : (a % FIRST + 1) * P].bitcast(FP8X4),
-                lhsT_scale=ea_plane[:, c, a * P : (a + 1) * P],
+                lhsT=ea[block // FIRST][:, c, block % FIRST * P : (block % FIRST + 1) * P].bitcast(FP8X4),
+                lhsT_scale=ea_plane[:, c, block * P : (block + 1) * P],
                 rhs=rhs,
                 rhs_scale=rhs_scale,
                 start=start,
                 stop=stop,
             )
 
+        def plane_of(first, rest, row0, g, c):
+            return first[row0:, c, :] if g == 0 else rest[row0:, c, cols(g - 1)]
+
         def mm_old(n):
             g = n // ROWS
             take_bank(("old", n))
             for c in range(PASSES):
-                plane = old_plane_first[:, c, :] if g == 0 else old_plane_rest[:, c, cols(g - 1)]
+                plane = plane_of(old_plane_first, old_plane_rest, 0, g, c)
                 mx(("old", n), n, c, old[g][:, c, :].bitcast(FP4X4), plane, c == 0, c == PASSES - 1)
 
         def mm_mid(n, c):
@@ -164,42 +175,47 @@ def tile_schur_window_block_k3_kernel(
             opens = n >= FIRST and c == 0
             if opens:
                 take_bank(("sum", n))
-            mx(("sum", n), n, c, mid[g][:, c, :].bitcast(FP8X4), mid_plane[MID_ROW:, c, cols(g)], opens, False)
+            plane = plane_of(mid_plane_first, mid_plane_rest, MID_ROW, g, c)
+            mx(("sum", n), n, c, mid[g][:, c, :].bitcast(FP8X4), plane, opens, False)
 
         def mm_new(n, c):
-            s = n // ROWS * PASSES + c
+            index = n // ROWS * PASSES + c
             opens = n < FIRST and c == 0
             if opens:
                 take_bank(("sum", n))
-            mx(("sum", n), n, c, new[s][:].bitcast(FP8X4), new_plane[s][:], opens, c == PASSES - 1)
+            mx(("sum", n), n, c, new[index][:].bitcast(FP8X4), new_plane[index][:], opens, c == PASSES - 1)
 
         def weigh_old(n):
-            nc.vector.tensor_tensor(out=half(n), in0=bank_of[("old", n)][:], in1=f_all[:, cols(n // ROWS)], op=ALU.mult)
+            nc.vector.tensor_tensor(
+                out=acc_of(n), in0=bank_of[("old", n)][:], in1=f_all[:, cols(n // ROWS)], op=ALU.mult
+            )
             give_back(("old", n))
 
-        def from_b(q, x0, x1, engine):
-            g, at = 2 * q // ROWS, 2 * q % ROWS * W
-            eng = nc.gpsimd if engine == "gpsimd" else nc.vector
-            eng.tensor_tensor(
-                out=acc[q][:, x0:x1], in0=b_sb[g][:, at + x0 : at + x1], in1=acc[q][:, x0:x1], op=ALU.subtract
+        def from_b(q, col0, col1, engine):
+            g, at = q // PAIRS_IN_GROUP, q % PAIRS_IN_GROUP * 2 * W
+            engine.tensor_tensor(
+                out=acc[q][:, col0:col1],
+                in0=b_sb[g][:, at + col0 : at + col1],
+                in1=acc[q][:, col0:col1],
+                op=ALU.subtract,
             )
 
         def finish(n):
-            out = y_last[:] if n == TILES - 1 else half(n)
-            nc.vector.tensor_tensor(out=out, in0=half(n), in1=bank_of[("sum", n)][:], op=ALU.subtract)
+            out = y_last[:] if n == TILES - 1 else acc_of(n)
+            nc.vector.tensor_tensor(out=out, in0=acc_of(n), in1=bank_of[("sum", n)][:], op=ALU.subtract)
             give_back(("sum", n))
 
         def round_y(n):
             nc.scalar.copy(
-                out=y_bf[n][:].rearrange("p (u j e) -> p u j e", u=2, e=2),
-                in_=half(n).rearrange("p (j u e) -> p u j e", u=2, e=2),
+                out=y_bf[n][:].rearrange("p (u x e) -> p u x e", u=2, e=2),
+                in_=acc_of(n).rearrange("p (x u e) -> p u x e", u=2, e=2),
             )
 
         def round_last(n):
             nc.vector.tensor_tensor(
-                out=y_bf[n][:].rearrange("p (u j e) -> p u j e", u=2, e=2),
-                in0=half(n).rearrange("p (j u e) -> p u j e", u=2, e=2),
-                in1=bank_of[("sum", n)][:].rearrange("p (j u e) -> p u j e", u=2, e=2),
+                out=y_bf[n][:].rearrange("p (u x e) -> p u x e", u=2, e=2),
+                in0=acc_of(n).rearrange("p (x u e) -> p u x e", u=2, e=2),
+                in1=bank_of[("sum", n)][:].rearrange("p (x u e) -> p u x e", u=2, e=2),
                 op=ALU.subtract,
             )
 
@@ -208,39 +224,45 @@ def tile_schur_window_block_k3_kernel(
             for h in range(count):
                 words = y_bf[n0 + h][:].bitcast(F32)
                 for u in range(2):
-                    o = (count * u + h) * P
-                    nc.tensor.transpose(bank[:, o : o + P], words[:, u * P : (u + 1) * P], ident[:])
+                    at = (count * u + h) * P
+                    nc.tensor.transpose(bank[:, at : at + P], words[:, u * P : (u + 1) * P], ident[:])
 
         def copy_turned(n0, count):
-            at = n0 % 2 * W
+            at = n0 % ROWS * W
             nc.scalar.copy(
-                out=y_t[n0 // 2][:, at : at + count * W].bitcast(F32).rearrange("p (m u) -> p m u", u=2),
+                out=y_t[n0 // ROWS][:, at : at + count * W].bitcast(F32).rearrange("p (m u) -> p m u", u=2),
                 in_=bank_of[("turn", n0)][:, : 2 * count * P].rearrange("p (u m) -> p m u", u=2),
             )
             give_back(("turn", n0))
 
         def quantize_y(n0, count):
-            g, m0, at = n0 // ROWS, n0 % ROWS * P, n0 % 2 * W
+            g, block = n0 // ROWS, n0 % ROWS
             nc.vector.quantize_mx(
-                out=out_words[g][:, m0 : m0 + count * P].bitcast(FP8X4),
-                scales=out_plane[g][:, m0 : m0 + count * P],
-                in_=y_t[n0 // 2][:, at : at + count * W],
+                out=out_words[g][:, block * P : (block + count) * P].bitcast(FP8X4),
+                scales=out_plane[g][:, block * P : (block + count) * P],
+                in_=y_t[g][:, block * W : (block + count) * W],
             )
 
+        def quantize_pairs(pairs):
+            if len(pairs) > 1 and pairs[0] // PAIRS_IN_GROUP == pairs[1] // PAIRS_IN_GROUP:
+                quantize_y(2 * pairs[0], 4)
+                pairs = pairs[2:]
+            for pair in pairs:
+                quantize_y(2 * pair, 2)
+
         def store_y(n0, count):
-            a = n0 % ROWS
-            dst = out_0[a * P : (a + count) * P, cols(n0 // ROWS)].rearrange("(h p) n -> p h n", p=P)
-            at = n0 % 2 * W
+            block, at = n0 % ROWS, n0 % 2 * W
+            dst = out_0[block * P : (block + count) * P, cols(n0 // ROWS)].rearrange("(h p) n -> p h n", p=P)
             src = y_last[:] if n0 == TILES - 1 else acc[n0 // 2][:, at : at + count * W]
             nc.sync.dma_start(out=dst, in_=src.rearrange("p (h n) -> p h n", n=W))
 
-        def store_words(g, m0, m1):
+        def store_words(g, row0, row1):
             dst = out_1[g].rearrange("p m t -> p (m t)").bitcast(I32)
-            nc.sync.dma_start(out=dst[:, m0:m1], in_=out_words[g][:, m0:m1].bitcast(I32))
+            nc.sync.dma_start(out=dst[:, row0:row1], in_=out_words[g][:, row0:row1].bitcast(I32))
 
         def store_plane(g, queues):
-            for quad in range(4):
-                queues[quad].dma_start(
+            for quad, queue in zip(QUADS, queues):
+                queue.dma_start(
                     out=out_2[g][4 * quad : 4 * quad + 4, :].bitcast(I32),
                     in_=out_plane[g][32 * quad : 32 * quad + 4, :].bitcast(I32),
                 )
@@ -250,8 +272,9 @@ def tile_schur_window_block_k3_kernel(
         zero(ea_plane)
         zero(old_plane_first)
         make_identity(nc, ident[:])
-        zero(mid_plane)
+        zero(mid_plane_first)
         zero(old_plane_rest)
+        zero(mid_plane_rest)
         load_ea(0)
         load_plane(ea_plane, 0, ea_scales)
         load_e(0, 0)
@@ -260,14 +283,15 @@ def tile_schur_window_block_k3_kernel(
         load_e(0, 1)
         load_ea(1)
         load_mid(0)
-        load_plane(mid_plane, MID_ROW, mid_scales)
+        load_plane(mid_plane_first, MID_ROW, mid_scales[:, :, :W])
         load_b(0, 0, 2)
         load_e(1, 0)
         load_b(0, 2, 4)
         load_plane(old_plane_rest, 0, old_scales[:, :, W:])
         load_old(1)
         load_e(1, 1)
-        load_b(0, 4, 6)
+        load_b(0, 4, ROWS)
+        load_plane(mid_plane_rest, MID_ROW, mid_scales[:, :, W:])
         load_mid(1)
         load_b(1, 0, ROWS)
         load_e(2, 0)
@@ -277,20 +301,12 @@ def tile_schur_window_block_k3_kernel(
         load_b(2, 0, ROWS)
 
         nc.vector.reciprocal(out=d_inv[:], in_=d_sb[:].rearrange("p c t -> p (c t)"))
+
         f_words = f_sb[:].rearrange("p g t -> p (g t)").bitcast(F32)
         f_banks = [take_bank(("f", 0)), take_bank(("f", 1))]
         for w in range(2 * GROUPS):
-            o = w % 4 * P
-            nc.tensor.transpose(f_banks[w // 4][:, o : o + P], f_words[:, w : w + 1].to_broadcast([P, P]), ident[:])
-
-        def spread_f(g):
-            o = g % 2 * 2 * P
-            nc.scalar.copy(
-                out=f_all[:, cols(g)].bitcast(F32).rearrange("p (j u) -> p j u", u=2),
-                in_=f_banks[g // 2][:, o : o + 2 * P].rearrange("p (u j) -> p j u", u=2),
-            )
-            if g > 0:
-                give_back(("f", g // 2))
+            at = w % 4 * P
+            nc.tensor.transpose(f_banks[w // 4][:, at : at + P], f_words[:, w : w + 1].to_broadcast([P, P]), ident[:])
 
         warm = take_bank("warm")
         give_back("warm")
@@ -304,17 +320,24 @@ def tile_schur_window_block_k3_kernel(
                 start=True,
                 stop=True,
             )
+
         for g in range(GROUPS):
-            spread_f(g)
+            at = g % 2 * 2 * P
+            nc.scalar.copy(
+                out=f_all[:, cols(g)].bitcast(F32).rearrange("p (x u) -> p x u", u=2),
+                in_=f_banks[g // 2][:, at : at + 2 * P].rearrange("p (u x) -> p x u", u=2),
+            )
+        give_back(("f", 0))
+        give_back(("f", 1))
+
         for n in range(FIRST):
             mm_old(n)
-        scale_rows(0, 0, "vector")
-        weave(0, 0, "scalar")
-        weave(0, 1, "vector")
-        scale_rows(0, 1, "vector")
+        scale_rows(0, 0)
+        weave(0, 0, W // 2, nc.scalar.copy)
+        weave(0, W // 2, W, nc.vector.tensor_copy)
+        scale_rows(0, 1)
         quantize_new(0, 0)
-        weave(1, 0, "scalar")
-        weave(1, 1, "scalar")
+        weave(1, 0, W, nc.scalar.copy)
         mm_old(FIRST)
         for n in range(FIRST):
             mm_new(n, 0)
@@ -325,85 +348,82 @@ def tile_schur_window_block_k3_kernel(
         for n in range(FIRST):
             mm_mid(n, 0)
             mm_mid(n, 1)
-        from_b(0, 0, 2 * W, "vector")
+        from_b(0, 0, 2 * W, nc.vector)
         quantize_new(0, 1)
-        scale_rows(1, 0, "vector")
+        scale_rows(1, 0)
 
-        TURN = {4: [0], 10: [1, 2], 13: [3, 4, 5], 15: [6]}
         for q in range(PAIRS):
-            a = 2 * q
-            g, k = a // ROWS + 1, q % (ROWS // 2)
-            prep = g < GROUPS
+            n0 = 2 * q
+            next_group, place = q // PAIRS_IN_GROUP + 1, q % PAIRS_IN_GROUP
+            weaving = next_group < GROUPS and place < PASSES
             last = q == PAIRS - 1
-            due = TURN.get(a - 1, []) + TURN.get(a, [])
-            for n in (a, a + 1):
-                if ROWS <= n + 3 < TILES - 1:
-                    mm_old(n + 3)
+            turned = TURN_AFTER.get(n0 - 1, []) + TURN_AFTER.get(n0, [])
+
+            for n in (n0, n0 + 1):
+                if ROWS <= n + LEAD < TILES - 1:
+                    mm_old(n + LEAD)
                 if n >= FIRST:
                     mm_mid(n, 0)
                     mm_new(n, 0)
                     mm_mid(n, 1)
                 if n == TILES - 1:
-                    turn(a - 2, 2)
+                    turn(n0 - 2, 2)
                 mm_new(n, 1)
-                for r in TURN.get(n, []):
-                    turn(2 * r, 2)
+                for pair in TURN_AFTER.get(n, []):
+                    turn(2 * pair, 2)
             if q == PAIRS - 3:
                 mm_old(TILES - 1)
-            if prep and k < PASSES:
-                weave(k, 0, "scalar")
-                weave(k, 1, "scalar")
-            for r in due:
-                copy_turned(2 * r, 2)
+
+            if weaving:
+                weave(place, 0, W, nc.scalar.copy)
+            for pair in turned:
+                copy_turned(2 * pair, 2)
+
             if q < PAIRS - 2:
-                weigh_old(a + 3)
-                from_b(q + 1, SPLIT, 2 * W, "gpsimd")
+                weigh_old(n0 + LEAD)
+                from_b(q + 1, SPLIT, 2 * W, nc.gpsimd)
             if 0 < q < PAIRS - 1:
-                from_b(q, 0, SPLIT, "vector")
-            if a + 4 < TILES:
-                weigh_old(a + 4)
-            finish(a)
+                from_b(q, 0, SPLIT, nc.vector)
+            if n0 + LEAD + 1 < TILES:
+                weigh_old(n0 + LEAD + 1)
+            finish(n0)
             if last:
-                for r in due:
-                    quantize_y(2 * r, 2)
+                quantize_pairs(turned)
                 store_words(GROUPS - 1, 0, 2 * P)
-            round_y(a)
-            if last:
-                copy_turned(a - 2, 2)
-            if last:
-                round_last(a + 1)
-            finish(a + 1)
-            if not last:
-                round_y(a + 1)
-            if q == PAIRS - 2:
-                from_b(q + 1, 0, SPLIT, "vector")
-            if prep and k == 0:
-                scale_rows(g, 1, "vector")
-            if g + 1 < GROUPS and k == 2:
-                scale_rows(g + 1, 0, "vector")
-            if not last:
-                for r in due:
-                    quantize_y(2 * r, 2)
-            if prep and k < PASSES:
-                quantize_new(g, k)
-            if q == PAIRS - 3:
-                weigh_old(TILES - 1)
-                from_b(PAIRS - 1, SPLIT, 2 * W, "gpsimd")
-            if last:
-                store_y(a, 1)
-                store_y(a + 1, 1)
+                round_y(n0)
+                copy_turned(n0 - 2, 2)
+                round_last(n0 + 1)
+                finish(n0 + 1)
+                store_y(n0, 1)
+                store_y(n0 + 1, 1)
             else:
-                store_y(a, 2)
-            for r in due:
-                if r % 3 == 2:
-                    store_words(r // 3, 0, M)
-                    store_plane(r // 3, [nc.sync] * 4)
-        turn(16, 1)
-        turn(17, 1)
-        copy_turned(16, 1)
-        copy_turned(17, 1)
-        quantize_y(14, 2)
-        quantize_y(16, 1)
-        quantize_y(17, 1)
-        store_words(2, 2 * P, 6 * P)
-        store_plane(2, [nc.scalar, nc.sync, nc.scalar, nc.sync])
+                round_y(n0)
+                finish(n0 + 1)
+                round_y(n0 + 1)
+                if q == PAIRS - 2:
+                    from_b(q + 1, 0, SPLIT, nc.vector)
+                if next_group < GROUPS and place == 0:
+                    scale_rows(next_group, 1)
+                if next_group + 1 < GROUPS and place == PAIRS_IN_GROUP - 1:
+                    scale_rows(next_group + 1, 0)
+                quantize_pairs(turned)
+                if weaving:
+                    quantize_new(next_group, place)
+                if q == PAIRS - 3:
+                    weigh_old(TILES - 1)
+                    from_b(PAIRS - 1, SPLIT, 2 * W, nc.gpsimd)
+                store_y(n0, 2)
+                for pair in turned:
+                    if pair % PAIRS_IN_GROUP == PAIRS_IN_GROUP - 1:
+                        store_words(pair // PAIRS_IN_GROUP, 0, M)
+                        store_plane(pair // PAIRS_IN_GROUP, [nc.sync] * 4)
+
+        for n in (TILES - 2, TILES - 1):
+            turn(n, 1)
+        for n in (TILES - 2, TILES - 1):
+            copy_turned(n, 1)
+        quantize_y(TILES - 4, 2)
+        for n in (TILES - 2, TILES - 1):
+            quantize_y(n, 1)
+        store_words(GROUPS - 1, 2 * P, M)
+        store_plane(GROUPS - 1, [nc.scalar, nc.sync, nc.scalar, nc.sync])

from contextlib import ExitStack

import concourse.mybir as mybir
from concourse.masks import make_identity

M, K, N = 768, 1024, 1536
FLOPS = 3 * 2 * M * K * N

F32 = mybir.dt.float32
BF16 = mybir.dt.bfloat16
I32 = mybir.dt.int32
U32 = mybir.dt.uint32
U8 = mybir.dt.uint8
FP8X4 = mybir.dt.float8_e4m3fn_x4
FP4X4 = mybir.dt.float4_e2m1fn_x4
ALU = mybir.AluOpType

P = 128
PACK = 4
W = 512
PASSES = K // (P * PACK)
GROUPS = N // W
ROWS = M // P
TILES = GROUPS * ROWS
PAIRS = TILES // 2
PAIRS_IN_GROUP = ROWS // 2
BANKS = 8
ALIGN = 256
FIRST = 3
LEAD = 3
MID_ROW = 4
QUADS = (0, 2, 1, 3)
WARM_PASSES = 6
SPLIT = 352
TURN_AFTER = {4: [0], 10: [1, 2], 13: [3, 4, 5], 15: [6]}


def tile_schur_window_block_k3_kernel(
    tc, ea_words, ea_scales, old_words, old_scales, mid_words, mid_scales, e_new, d, f, b, out_0, out_1, out_2
):
    nc = tc.nc
    with ExitStack() as ctx:
        sb = ctx.enter_context(tc.tile_pool(name="sb", bufs=1))
        ps = ctx.enter_context(tc.psum_pool(name="ps", bufs=1))
        ctx.enter_context(tc.manual_schedule())

        def tile(name, shape, dtype):
            return sb.tile(shape, dtype, name=name, align_bytes=ALIGN)

        def tiles(name, count, shape, dtype):
            return [tile("%s%d" % (name, i), shape, dtype) for i in range(count)]

        banks = [ps.tile([P, W], F32, name="bank%d" % i) for i in range(BANKS)]
        ident = tile("ident", [P, P], F32)
        d_sb = tile("d_sb", [P, PASSES, PACK], BF16)
        d_inv = tile("d_inv", [P, PASSES * PACK], F32)
        f_sb = tile("f_sb", [P, GROUPS, PACK], BF16)
        f_all = tile("f_all", [P, N], BF16)
        ea_plane = tile("ea_plane", [P, PASSES, M], U8)
        old_plane_first = tile("old_plane_first", [P, PASSES, W], U8)
        old_plane_rest = tile("old_plane_rest", [P, PASSES, N - W], U8)
        mid_plane_first = tile("mid_plane_first", [P, PASSES, W], U8)
        mid_plane_rest = tile("mid_plane_rest", [P, PASSES, N - W], U8)
        ea = tiles("ea", ROWS // FIRST, [P, PASSES, FIRST * P], U32)
        old = tiles("old", GROUPS, [P, PASSES, 2 * W], U8)
        mid = tiles("mid", GROUPS, [P, PASSES, W], U32)
        raw = tiles("raw", GROUPS * PASSES, [P, PACK, W], BF16)
        scaled = tiles("scaled", PASSES, [P, PACK, W], BF16)
        woven = tiles("woven", PASSES, [P, W, PACK], BF16)
        new = tiles("new", GROUPS * PASSES, [P, W], U32)
        new_plane = tiles("new_plane", GROUPS * PASSES, [P, W], U8)
        b_sb = tiles("b_sb", GROUPS, [P, ROWS * W], BF16)
        acc = tiles("acc", PAIRS, [P, 2 * W], F32)
        y_last = tile("y_last", [P, W], F32)
        y_bf = tiles("y_bf", TILES, [P, W], BF16)
        y_t = tiles("y_t", GROUPS, [P, M * PACK], BF16)
        out_words = tiles("out_words", GROUPS, [P, M], U32)
        out_plane = tiles("out_plane", GROUPS, [P, M], U8)

        free_banks = list(banks)
        bank_of = {}

        def take_bank(key):
            bank_of[key] = free_banks.pop(0)
            return bank_of[key]

        def give_back(key):
            free_banks.append(bank_of[key])

        def cols(index):
            return slice(index * W, (index + 1) * W)

        def acc_of(n):
            return acc[n // 2][:, cols(n % 2)]

        ea_src = ea_words.rearrange("c p m t -> p c (m t)").bitcast(I32)
        old_src = old_words.rearrange("c p x -> p c x").bitcast(I32)
        mid_src = mid_words.rearrange("c p n t -> p c (n t)").bitcast(I32)
        e_src = e_new.rearrange("(c p t) n -> c p t n", p=P, t=PACK)
        b_src = b.rearrange("(a p) n -> p a n", p=P)

        def load_ea(part):
            span = slice(part * FIRST * P, (part + 1) * FIRST * P)
            nc.sync.dma_start(out=ea[part][:].bitcast(I32), in_=ea_src[:, :, span])

        def load_old(g):
            nc.sync.dma_start(out=old[g][:].bitcast(I32), in_=old_src[:, :, g * W // 2 : (g + 1) * W // 2])

        def load_mid(g):
            nc.sync.dma_start(out=mid[g][:].bitcast(I32), in_=mid_src[:, :, cols(g)])

        def load_e(g, c):
            nc.sync.dma_start(out=raw[g * PASSES + c][:], in_=e_src[c][:, :, cols(g)])

        def load_b(g, block0, block1):
            dst = b_sb[g][:].rearrange("p (a n) -> p a n", n=W)
            nc.sync.dma_start(out=dst[:, block0:block1, :], in_=b_src[:, block0:block1, cols(g)])

        def zero(plane):
            nc.vector.memset(plane[:].rearrange("p c n -> p (c n)").bitcast(I32), 0)

        def load_plane(plane, row0, scales):
            src = scales.rearrange("c q n -> q c n").bitcast(I32)
            for quad in QUADS:
                row = 32 * quad + row0
                nc.sync.dma_start(out=plane[row : row + 4, :, :].bitcast(I32), in_=src[4 * quad : 4 * quad + 4])

        def scale_rows(g, c):
            for t in range(PACK):
                nc.vector.tensor_scalar(
                    out=scaled[c][:, t, :],
                    in0=raw[g * PASSES + c][:, t, :],
                    scalar1=d_inv[:, c * PACK + t : c * PACK + t + 1],
                    scalar2=None,
                    op0=ALU.mult,
                )

        def weave(c, col0, col1, copy):
            copy(
                out=woven[c][:, col0:col1, :].rearrange("p (x i) t -> p x t i", i=4),
                in_=scaled[c][:, :, col0:col1].rearrange("p t (x i) -> p x t i", i=4),
            )

        def quantize_new(g, c):
            nc.vector.quantize_mx(
                out=new[g * PASSES + c][:].bitcast(FP8X4),
                scales=new_plane[g * PASSES + c][:],
                in_=woven[c][:].rearrange("p w t -> p (w t)"),
            )

        def mx(key, n, c, rhs, rhs_scale, start, stop):
            block = n % ROWS
            nc.tensor.matmul_mx(
                out=bank_of[key][:],
                lhsT=ea[block // FIRST][:, c, block % FIRST * P : (block % FIRST + 1) * P].bitcast(FP8X4),
                lhsT_scale=ea_plane[:, c, block * P : (block + 1) * P],
                rhs=rhs,
                rhs_scale=rhs_scale,
                start=start,
                stop=stop,
            )

        def plane_of(first, rest, row0, g, c):
            return first[row0:, c, :] if g == 0 else rest[row0:, c, cols(g - 1)]

        def mm_old(n):
            g = n // ROWS
            take_bank(("old", n))
            for c in range(PASSES):
                plane = plane_of(old_plane_first, old_plane_rest, 0, g, c)
                mx(("old", n), n, c, old[g][:, c, :].bitcast(FP4X4), plane, c == 0, c == PASSES - 1)

        def mm_mid(n, c):
            g = n // ROWS
            opens = n >= FIRST and c == 0
            if opens:
                take_bank(("sum", n))
            plane = plane_of(mid_plane_first, mid_plane_rest, MID_ROW, g, c)
            mx(("sum", n), n, c, mid[g][:, c, :].bitcast(FP8X4), plane, opens, False)

        def mm_new(n, c):
            index = n // ROWS * PASSES + c
            opens = n < FIRST and c == 0
            if opens:
                take_bank(("sum", n))
            mx(("sum", n), n, c, new[index][:].bitcast(FP8X4), new_plane[index][:], opens, c == PASSES - 1)

        def weigh_old(n):
            nc.vector.tensor_tensor(
                out=acc_of(n), in0=bank_of[("old", n)][:], in1=f_all[:, cols(n // ROWS)], op=ALU.mult
            )
            give_back(("old", n))

        def from_b(q, col0, col1, engine):
            g, at = q // PAIRS_IN_GROUP, q % PAIRS_IN_GROUP * 2 * W
            engine.tensor_tensor(
                out=acc[q][:, col0:col1],
                in0=b_sb[g][:, at + col0 : at + col1],
                in1=acc[q][:, col0:col1],
                op=ALU.subtract,
            )

        def finish(n):
            out = y_last[:] if n == TILES - 1 else acc_of(n)
            nc.vector.tensor_tensor(out=out, in0=acc_of(n), in1=bank_of[("sum", n)][:], op=ALU.subtract)
            give_back(("sum", n))

        def round_y(n):
            nc.scalar.copy(
                out=y_bf[n][:].rearrange("p (u x e) -> p u x e", u=2, e=2),
                in_=acc_of(n).rearrange("p (x u e) -> p u x e", u=2, e=2),
            )

        def round_last(n):
            nc.vector.tensor_tensor(
                out=y_bf[n][:].rearrange("p (u x e) -> p u x e", u=2, e=2),
                in0=acc_of(n).rearrange("p (x u e) -> p u x e", u=2, e=2),
                in1=bank_of[("sum", n)][:].rearrange("p (x u e) -> p u x e", u=2, e=2),
                op=ALU.subtract,
            )

        def turn(n0, count):
            bank = take_bank(("turn", n0))
            for h in range(count):
                words = y_bf[n0 + h][:].bitcast(F32)
                for u in range(2):
                    at = (count * u + h) * P
                    nc.tensor.transpose(bank[:, at : at + P], words[:, u * P : (u + 1) * P], ident[:])

        def copy_turned(n0, count):
            at = n0 % ROWS * W
            nc.scalar.copy(
                out=y_t[n0 // ROWS][:, at : at + count * W].bitcast(F32).rearrange("p (m u) -> p m u", u=2),
                in_=bank_of[("turn", n0)][:, : 2 * count * P].rearrange("p (u m) -> p m u", u=2),
            )
            give_back(("turn", n0))

        def quantize_y(n0, count):
            g, block = n0 // ROWS, n0 % ROWS
            nc.vector.quantize_mx(
                out=out_words[g][:, block * P : (block + count) * P].bitcast(FP8X4),
                scales=out_plane[g][:, block * P : (block + count) * P],
                in_=y_t[g][:, block * W : (block + count) * W],
            )

        def quantize_pairs(pairs):
            if len(pairs) > 1 and pairs[0] // PAIRS_IN_GROUP == pairs[1] // PAIRS_IN_GROUP:
                quantize_y(2 * pairs[0], 4)
                pairs = pairs[2:]
            for pair in pairs:
                quantize_y(2 * pair, 2)

        def store_y(n0, count):
            block, at = n0 % ROWS, n0 % 2 * W
            dst = out_0[block * P : (block + count) * P, cols(n0 // ROWS)].rearrange("(h p) n -> p h n", p=P)
            src = y_last[:] if n0 == TILES - 1 else acc[n0 // 2][:, at : at + count * W]
            nc.sync.dma_start(out=dst, in_=src.rearrange("p (h n) -> p h n", n=W))

        def store_words(g, row0, row1):
            dst = out_1[g].rearrange("p m t -> p (m t)").bitcast(I32)
            nc.sync.dma_start(out=dst[:, row0:row1], in_=out_words[g][:, row0:row1].bitcast(I32))

        def store_plane(g, queues):
            for quad, queue in zip(QUADS, queues):
                queue.dma_start(
                    out=out_2[g][4 * quad : 4 * quad + 4, :].bitcast(I32),
                    in_=out_plane[g][32 * quad : 32 * quad + 4, :].bitcast(I32),
                )

        nc.sync.dma_start(out=d_sb[:], in_=d.rearrange("(c p t) -> p c t", p=P, t=PACK))
        nc.sync.dma_start(out=f_sb[:], in_=f.rearrange("(g p t) -> p g t", p=P, t=PACK))
        zero(ea_plane)
        zero(old_plane_first)
        make_identity(nc, ident[:])
        zero(mid_plane_first)
        zero(old_plane_rest)
        zero(mid_plane_rest)
        load_ea(0)
        load_plane(ea_plane, 0, ea_scales)
        load_e(0, 0)
        load_old(0)
        load_plane(old_plane_first, 0, old_scales[:, :, :W])
        load_e(0, 1)
        load_ea(1)
        load_mid(0)
        load_plane(mid_plane_first, MID_ROW, mid_scales[:, :, :W])
        load_b(0, 0, 2)
        load_e(1, 0)
        load_b(0, 2, 4)
        load_plane(old_plane_rest, 0, old_scales[:, :, W:])
        load_old(1)
        load_e(1, 1)
        load_b(0, 4, ROWS)
        load_plane(mid_plane_rest, MID_ROW, mid_scales[:, :, W:])
        load_mid(1)
        load_b(1, 0, ROWS)
        load_e(2, 0)
        load_e(2, 1)
        load_old(2)
        load_mid(2)
        load_b(2, 0, ROWS)

        nc.vector.reciprocal(out=d_inv[:], in_=d_sb[:].rearrange("p c t -> p (c t)"))

        f_words = f_sb[:].rearrange("p g t -> p (g t)").bitcast(F32)
        f_banks = [take_bank(("f", 0)), take_bank(("f", 1))]
        for w in range(2 * GROUPS):
            at = w % 4 * P
            nc.tensor.transpose(f_banks[w // 4][:, at : at + P], f_words[:, w : w + 1].to_broadcast([P, P]), ident[:])

        warm = take_bank("warm")
        give_back("warm")
        for i in range(WARM_PASSES):
            nc.tensor.matmul_mx(
                out=warm[:, : 2 * P],
                lhsT=ea[0][:, 0, :P].bitcast(FP8X4),
                lhsT_scale=ea_plane[:, 0, :P],
                rhs=ea[0][:, 0, : 2 * P].bitcast(FP8X4),
                rhs_scale=ea_plane[:, 0, : 2 * P],
                start=True,
                stop=True,
            )

        for g in range(GROUPS):
            at = g % 2 * 2 * P
            nc.scalar.copy(
                out=f_all[:, cols(g)].bitcast(F32).rearrange("p (x u) -> p x u", u=2),
                in_=f_banks[g // 2][:, at : at + 2 * P].rearrange("p (u x) -> p x u", u=2),
            )
        give_back(("f", 0))
        give_back(("f", 1))

        for n in range(FIRST):
            mm_old(n)
        scale_rows(0, 0)
        weave(0, 0, W // 2, nc.scalar.copy)
        weave(0, W // 2, W, nc.vector.tensor_copy)
        scale_rows(0, 1)
        quantize_new(0, 0)
        weave(1, 0, W, nc.scalar.copy)
        mm_old(FIRST)
        for n in range(FIRST):
            mm_new(n, 0)
        for n in range(FIRST):
            weigh_old(n)
        for n in range(FIRST + 1, ROWS):
            mm_old(n)
        for n in range(FIRST):
            mm_mid(n, 0)
            mm_mid(n, 1)
        from_b(0, 0, 2 * W, nc.vector)
        quantize_new(0, 1)
        scale_rows(1, 0)

        for q in range(PAIRS):
            n0 = 2 * q
            next_group, place = q // PAIRS_IN_GROUP + 1, q % PAIRS_IN_GROUP
            weaving = next_group < GROUPS and place < PASSES
            last = q == PAIRS - 1
            turned = TURN_AFTER.get(n0 - 1, []) + TURN_AFTER.get(n0, [])

            for n in (n0, n0 + 1):
                if ROWS <= n + LEAD < TILES - 1:
                    mm_old(n + LEAD)
                if n >= FIRST:
                    mm_mid(n, 0)
                    mm_new(n, 0)
                    mm_mid(n, 1)
                if n == TILES - 1:
                    turn(n0 - 2, 2)
                mm_new(n, 1)
                for pair in TURN_AFTER.get(n, []):
                    turn(2 * pair, 2)
            if q == PAIRS - 3:
                mm_old(TILES - 1)

            if weaving:
                weave(place, 0, W, nc.scalar.copy)
            for pair in turned:
                copy_turned(2 * pair, 2)

            if q < PAIRS - 2:
                weigh_old(n0 + LEAD)
                from_b(q + 1, SPLIT, 2 * W, nc.gpsimd)
            if 0 < q < PAIRS - 1:
                from_b(q, 0, SPLIT, nc.vector)
            if n0 + LEAD + 1 < TILES:
                weigh_old(n0 + LEAD + 1)
            finish(n0)
            if last:
                quantize_pairs(turned)
                store_words(GROUPS - 1, 0, 2 * P)
                round_y(n0)
                copy_turned(n0 - 2, 2)
                round_last(n0 + 1)
                finish(n0 + 1)
                store_y(n0, 1)
                store_y(n0 + 1, 1)
            else:
                round_y(n0)
                finish(n0 + 1)
                round_y(n0 + 1)
                if q == PAIRS - 2:
                    from_b(q + 1, 0, SPLIT, nc.vector)
                if next_group < GROUPS and place == 0:
                    scale_rows(next_group, 1)
                if next_group + 1 < GROUPS and place == PAIRS_IN_GROUP - 1:
                    scale_rows(next_group + 1, 0)
                quantize_pairs(turned)
                if weaving:
                    quantize_new(next_group, place)
                if q == PAIRS - 3:
                    weigh_old(TILES - 1)
                    from_b(PAIRS - 1, SPLIT, 2 * W, nc.gpsimd)
                store_y(n0, 2)
                for pair in turned:
                    if pair % PAIRS_IN_GROUP == PAIRS_IN_GROUP - 1:
                        store_words(pair // PAIRS_IN_GROUP, 0, M)
                        store_plane(pair // PAIRS_IN_GROUP, [nc.sync] * 4)

        for n in (TILES - 2, TILES - 1):
            turn(n, 1)
        for n in (TILES - 2, TILES - 1):
            copy_turned(n, 1)
        quantize_y(TILES - 4, 2)
        for n in (TILES - 2, TILES - 1):
            quantize_y(n, 1)
        store_words(GROUPS - 1, 2 * P, M)
        store_plane(GROUPS - 1, [nc.scalar, nc.sync, nc.scalar, nc.sync])
